import numpy as np
import ml_dtypes


def mxq(x, axis, fmt="e4m3"):
    dtype, down = {"e4m3": (ml_dtypes.float8_e4m3fn, 7), "e5m2": (ml_dtypes.float8_e5m2, 14)}[fmt]
    v = np.moveaxis(np.asarray(x, np.float32).astype(ml_dtypes.bfloat16).astype(np.float64), axis, -1)
    blocks = v.reshape(v.shape[:-1] + (-1, 32))
    amax = np.abs(blocks).max(-1, keepdims=True)
    byte = np.maximum(np.where(amax > 0, np.frexp(amax)[1] - 1 + 127, 0) - down, 1)
    scale = np.exp2(byte - 127.0)
    codes = (blocks / scale).astype(np.float32).astype(dtype).astype(np.float64)
    return np.moveaxis((codes * scale).reshape(v.shape), -1, axis)


WIDE = False


def mx_kscale(k):
    if not WIDE:
        return np.ones(k)
    levels = np.array([10, -10, 5, -5, 0])
    if k % 512:
        return np.exp2(np.random.permutation(np.resize(levels, k // 32))).repeat(32)
    a = np.empty((k // 512, 16))
    for p in range(k // 512):
        a[p, :8] = np.random.permutation(np.resize(levels, 8))
        for g in range(8):
            far = levels[np.abs(levels - a[p, g]) >= 10]
            a[p, g + 8] = far[np.random.randint(len(far))]
    return np.exp2(a.ravel()).repeat(32)


def f64(x):
    return np.asarray(x).astype(np.float64)


def striped(idx):
    return np.tile(idx.reshape(-1, 16).T, (8, 1)).astype(np.uint16)


def unstriped(offs):
    return offs[:16].T.reshape(-1).astype(np.int64)


E2M1 = np.array([0.0, 0.5, 1.0, 1.5, 2.0, 3.0, 4.0, 6.0, -0.0, -0.5, -1.0, -1.5, -2.0, -3.0, -4.0, -6.0])


def pack_weight(w, fmt):
    k, n = w.shape
    w = f64(np.asarray(w, np.float32).astype(ml_dtypes.bfloat16)).reshape(k // 32, 32, n)
    amax = np.abs(w).max(1)
    if fmt == "e4m3":
        byte = np.frexp(amax)[1] - 1 + 127 - 7
    else:
        mant, ex = np.frexp(amax / 6.0)
        byte = np.where(mant > 0.5, ex, ex - 1) + 127
    byte = np.clip(np.where(amax > 0, byte, 1), 1, 254)
    scaled = (w * np.exp2(127.0 - byte)[:, None, :]).reshape(k, n).astype(np.float32)
    by_word = np.ascontiguousarray(scaled.reshape(k // 512, 128, 4, n).transpose(0, 1, 3, 2))
    if fmt == "e4m3":
        words = by_word.astype(ml_dtypes.float8_e4m3fn).view(np.uint8)
    else:
        c = by_word.astype(ml_dtypes.float4_e2m1fn).view(np.uint8) & 0xF
        words = (c[..., 0::2] | (c[..., 1::2] << 4)).reshape(k // 512, 128, 2 * n)
    return np.ascontiguousarray(words), np.ascontiguousarray(byte.astype(np.uint8).reshape(k // 512, 16, n))


def unpack_weight(words, scales, fmt):
    g, _, n = scales.shape
    words = np.ascontiguousarray(words).reshape(g, 128, n, -1)
    if fmt == "e4m3":
        vals = words.view(ml_dtypes.float8_e4m3fn).astype(np.float64)
    else:
        nib = np.empty((g, 128, n, 4), np.uint8)
        nib[..., 0::2] = words & 0xF
        nib[..., 1::2] = words >> 4
        vals = E2M1[nib]
    vals = vals * np.repeat(np.exp2(scales.astype(np.float64) - 127.0), 8, axis=1)[..., None]
    return vals.transpose(0, 1, 3, 2).reshape(g * 512, n)


def silu(v):
    return v / (1.0 + np.exp(-np.maximum(v, -700.0)))


K, T, E, C, H, N = 512, 512, 8, 256, 512, 128
TOP = 4


def by_expert(wq, xq):
    return np.concatenate([wq[e].T @ xq[:, e * C:(e + 1) * C] for e in range(E)], axis=1)


def setup_inputs():
    n = np.random.standard_normal
    s = mx_kscale(K)[:, None]
    u = mx_kscale(H)
    deal = np.repeat(np.arange(E), C).reshape(TOP, T)[:, np.random.permutation(T)]
    deal = np.take_along_axis(deal, np.argsort(np.random.rand(TOP, T), axis=0), axis=0)
    for _ in range(8):
        s_, t_ = np.random.permutation(T).reshape(2, -1); r = np.random.randint(TOP, size=T // 2); x, y = deal[r, s_].copy(), deal[r, t_].copy()
        ok = ~((deal[:, s_] == y).any(0) | (deal[:, t_] == x).any(0)); deal[r[ok], s_[ok]] = y[ok]; deal[r[ok], t_[ok]] = x[ok]
    order = np.lexsort((np.random.rand(TOP * T), deal.reshape(-1)))
    slot_token = order % T; pos = np.empty(TOP * T, np.int64); pos[order] = np.arange(TOP * T); pos = pos.reshape(TOP, T)
    g = np.random.uniform(0.5, 1.5, (TOP, T)); g = g / g.sum(0)
    w1 = [pack_weight(m, "e2m1") for m in n((E, K, H)) / np.sqrt(K) / s[None]]
    w3 = [pack_weight(m, "e2m1") for m in n((E, K, H)) / np.sqrt(K) / s[None] * u[None, None, :]]
    w2 = [pack_weight(m, "e2m1") for m in n((E, H, N)) / np.sqrt(H) / u[None, :, None]]
    return {
        "xT": (n((K, T)) * s).astype(np.float32),
        "w1_words": np.stack([m[0] for m in w1]),
        "w1_scales": np.stack([m[1] for m in w1]),
        "w3_words": np.stack([m[0] for m in w3]),
        "w3_scales": np.stack([m[1] for m in w3]),
        "w2_words": np.stack([m[0] for m in w2]),
        "w2_scales": np.stack([m[1] for m in w2]),
        "gate": np.stack([np.tile(r, (N, 1)) for r in g]).astype(np.float32),
        "offs": striped(slot_token),
        "pos1": striped(pos[0]),
        "pos2": striped(pos[1]),
        "pos3": striped(pos[2]),
        "pos4": striped(pos[3]),
    }


def reference(xT, w1_words, w1_scales, w3_words, w3_scales, w2_words, w2_scales, gate, offs, pos1, pos2, pos3, pos4):
    idx = unstriped(offs)
    w1 = np.stack([unpack_weight(w1_words[e], w1_scales[e], "e2m1") for e in range(E)])
    w3 = np.stack([unpack_weight(w3_words[e], w3_scales[e], "e2m1") for e in range(E)])
    w2 = np.stack([unpack_weight(w2_words[e], w2_scales[e], "e2m1") for e in range(E)])
    xq = mxq(f64(xT)[:, idx], 0, "e4m3")
    h = silu(by_expert(w1, xq))
    h = h * by_expert(w3, xq)
    y = by_expert(w2, mxq(h, 0, "e4m3"))
    return sum(f64(gate[r]) * y[:, unstriped(p)] for r, p in enumerate((pos1, pos2, pos3, pos4)))

@@ -1,0 +1,247 @@
+from contextlib import ExitStack
+
+import concourse.mybir as mybir
+from concourse.masks import make_identity
+
+T, E, C, K, H, N, TOP = 512, 8, 256, 512, 512, 128, 4
+P = 128
+S = E * C
+FLOPS = 2 * S * (2 * K * H + H * N)
+
+F32 = mybir.dt.float32
+BF16 = mybir.dt.bfloat16
+I32 = mybir.dt.int32
+U32 = mybir.dt.uint32
+U16 = mybir.dt.uint16
+U8 = mybir.dt.uint8
+FP8X4 = mybir.dt.float8_e4m3fn_x4
+FP4X4 = mybir.dt.float4_e2m1fn_x4
+SILU = mybir.ActivationFunctionType.Silu
+ADD = mybir.AluOpType.add
+MULT = mybir.AluOpType.mult
+
+
+def tile_moe_tk_glu_silu_kernel(
+    tc, xT, w1_words, w1_scales, w3_words, w3_scales, w2_words, w2_scales, gate, offs, pos1, pos2, pos3, pos4, out
+):
+    nc = tc.nc
+    with ExitStack() as ctx:
+        keep = ctx.enter_context(tc.tile_pool(name="keep", bufs=1))
+        flow = ctx.enter_context(tc.tile_pool(name="flow", bufs=4))
+        psum_a = ctx.enter_context(tc.psum_pool(name="psum_a", bufs=2))
+        psum_b = ctx.enter_context(tc.psum_pool(name="psum_b", bufs=3))
+        psum_t = ctx.enter_context(tc.psum_pool(name="psum_t", bufs=2))
+        psum_y = ctx.enter_context(tc.psum_pool(name="psum_y", bufs=1))
+
+        offsets = keep.tile([P, S // 16], U16, name="offsets")
+        positions = [keep.tile([P, T // 16], U16, name=f"positions{r}") for r in range(TOP)]
+        x_raw = keep.tile([P, 4, T], F32, name="x_raw")
+        x_rows = keep.tile([P, T, 4], BF16, name="x_rows", align_bytes=64)
+        x_codes = keep.tile([P, T], U32, name="x_codes", align_bytes=64)
+        x_scales = keep.tile([P, T], U8, name="x_scales", align_bytes=64)
+        gates = keep.tile([P, TOP, T], F32, name="gates")
+        y_all = keep.tile([P, S], F32, name="y_all")
+        ident = keep.tile([P, P], F32, name="ident")
+        one = keep.tile([P, 1], F32, name="one")
+
+        plane1 = keep.tile([P, E, H], U8, name="plane1", align_bytes=64)
+        plane3 = keep.tile([P, E, H], U8, name="plane3", align_bytes=64)
+        plane2 = keep.tile([P, E, N], U8, name="plane2", align_bytes=64)
+        words1 = [keep.tile([P, 2, 2 * H], U8, name=f"words1_{i}", align_bytes=64) for i in range(E // 2)]
+        words3 = [keep.tile([P, 2, 2 * H], U8, name=f"words3_{i}", align_bytes=64) for i in range(E // 2)]
+        words2 = keep.tile([P, E, 2 * N], U8, name="words2", align_bytes=64)
+
+        def zero(plane):
+            nc.vector.memset(plane[:].rearrange("p e i -> p (e i)").bitcast(I32), 0)
+
+        def load_plane(plane, scales, lo, hi):
+            rows = scales.bitcast(I32).rearrange("e s (q r) i -> r q (e s) i", r=4)
+            for r in range(4):
+                nc.sync.dma_start(plane[r:P:32, :, :].bitcast(I32), rows[r][:, lo:hi, :])
+
+        def load_words(tile, words, lo, hi):
+            nc.sync.dma_start(tile[:].bitcast(I32), words.bitcast(I32).rearrange("e s p i -> p (e s) i")[:, lo:hi, :])
+
+        x_view = xT.rearrange("(p j) t -> p j t", j=4)
+        half = T // 2
+        for i in range(2):
+            cols = slice(i * half, (i + 1) * half)
+            nc.sync.dma_start(x_raw[:, :, cols], x_view[:, :, cols])
+        nc.sync.dma_start(offsets[:], offs)
+        nc.vector.memset(one[:], 0.0)
+        nc.scalar.activation(one[:], one[:], SILU)
+        zero(plane1)
+        zero(plane3)
+        zero(plane2)
+        nc.gpsimd.memset(x_scales[:], 0)
+        make_identity(nc, ident[:])
+        load_plane(plane1, w1_scales, 0, E)
+        load_words(words1[0], w1_words, 0, 2)
+        load_words(words3[0], w3_words, 0, 2)
+        load_plane(plane3, w3_scales, 0, E)
+        load_words(words1[1], w1_words, 2, 4)
+        load_words(words3[1], w3_words, 2, 4)
+        load_plane(plane2, w2_scales, 0, E)
+        load_words(words2, w2_words, 0, E)
+        for i in range(2, E // 2):
+            load_words(words1[i], w1_words, 2 * i, 2 * i + 2)
+            load_words(words3[i], w3_words, 2 * i, 2 * i + 2)
+        for tile, pos in zip(positions, (pos1, pos2, pos3, pos4)):
+            nc.sync.dma_start(tile[:], pos)
+        nc.sync.dma_start(gates[:], gate.rearrange("r p t -> p r t"))
+
+        def interleave(copy, lo, hi):
+            copy(x_rows[:, lo:hi, :], x_raw[:, :, lo:hi].rearrange("p j t -> p t j"))
+
+        def quantise(lo, hi):
+            nc.vector.quantize_mx(
+                out=x_codes[:, lo:hi].bitcast(FP8X4),
+                scales=x_scales[:, lo:hi],
+                in_=x_rows[:, lo:hi, :].rearrange("p t j -> p (t j)"),
+            )
+
+        interleave(nc.scalar.copy, 0, 128)
+        interleave(nc.vector.tensor_copy, 128, 256)
+        quantise(128, 256)
+        quantise(0, 128)
+        interleave(nc.scalar.copy, 448, 512)
+        interleave(nc.vector.tensor_copy, 256, 384)
+        interleave(nc.vector.tensor_copy, 384, 448)
+        quantise(256, 384)
+        quantise(384, 512)
+
+        gathered = {}
+        runs = [(0, 128), (128, 512), (512, 896), (896, 1280), (1280, 1664), (1664, 2048)]
+        first = {}
+        hidden = {}
+        turned = {}
+        on_gpsimd = ()
+
+        def gather(g):
+            lo, hi = runs[g]
+            codes = flow.tile([P, hi - lo], U32, name="codes", align_bytes=64)
+            scales = flow.tile([P, hi - lo], U8, name="scales", align_bytes=64)
+            mine = offsets[:, lo // 16 : hi // 16]
+            nc.vector.tensor_copy(codes[:], x_codes[:].indirect(mine))
+            nc.vector.tensor_copy(scales[:], x_scales[:].indirect(mine))
+            for t in range(lo // P, hi // P):
+                cols = slice(t * P - lo, t * P - lo + P)
+                gathered[t] = (codes[:, cols], scales[:, cols])
+
+        def layer1(e, s):
+            codes, scales = gathered.pop(2 * e + s)
+            a = psum_a.tile([P, H], F32, name="a")
+            b = psum_b.tile([P, H], F32, name="b")
+            for bank, words, plane in ((a, words1, plane1), (b, words3, plane3)):
+                nc.tensor.matmul_mx(
+                    out=bank[:],
+                    lhsT=codes.bitcast(FP8X4),
+                    lhsT_scale=scales,
+                    rhs=words[e // 2][:, e % 2, :].bitcast(FP4X4),
+                    rhs_scale=plane[:, e, :],
+                    start=True,
+                    stop=True,
+                )
+            first[e, s] = (a, b)
+
+        def split(t):
+            return t[:].rearrange("p (m u d) -> p u m d", u=2, d=2)
+
+        def pieces(t):
+            return t[:].rearrange("p (u m d) -> p u m d", u=2, d=2)
+
+        def glu(e, s):
+            a, b = first.pop((e, s))
+            h = flow.tile([P, H], BF16, name="h", align_bytes=64)
+            sa = flow.tile([P, H], F32, name="sa")
+            if (e, s) in on_gpsimd:
+                sb = flow.tile([P, H], F32, name="sb")
+                nc.scalar.copy(pieces(sb), split(b))
+                nc.scalar.activation(pieces(sa), split(a), SILU)
+                nc.gpsimd.tensor_tensor(h[:], sb[:], sa[:], MULT)
+            else:
+                nc.scalar.activation(pieces(sa), split(a), SILU)
+                nc.vector.tensor_tensor(pieces(h), split(b), pieces(sa), MULT)
+            hidden[e, s] = h
+
+        def turn(e, tiles, copy):
+            n = len(tiles)
+            bank = psum_t.tile([P, n, 2, P], F32, name="bank")
+            for i, s in enumerate(tiles):
+                h = hidden.pop((e, s))
+                for u in range(2):
+                    nc.tensor.transpose(bank[:, i, u, :], h[:, u * 256 : (u + 1) * 256].bitcast(F32), ident[:])
+            rows = flow.tile([P, n * P * 4], BF16, name="rows", align_bytes=64)
+            copy(
+                rows[:].bitcast(F32).rearrange("p (s c u) -> p s c u", s=n, u=2), bank[:].rearrange("p s u c -> p s c u")
+            )
+            turned[e, tiles] = rows
+
+        def layer2(e, tiles, pool, name, copy):
+            rows = turned.pop((e, tiles))
+            n = len(tiles) * P
+            hc = flow.tile([P, n], U32, name="hc", align_bytes=64)
+            hs = flow.tile([P, n], U8, name="hs", align_bytes=64)
+            nc.vector.quantize_mx(out=hc[:].bitcast(FP8X4), scales=hs[:], in_=rows[:])
+            y = pool.tile([P, n], F32, name=name)
+            nc.tensor.matmul_mx(
+                out=y[:],
+                lhsT=words2[:, e, :].bitcast(FP4X4),
+                lhsT_scale=plane2[:, e, :],
+                rhs=hc[:].bitcast(FP8X4),
+                rhs_scale=hs[:],
+                start=True,
+                stop=True,
+            )
+            lo = e * C + tiles[0] * P
+            copy(y_all[:, lo : lo + n], y[:])
+
+        both = (0, 1)
+        last = E - 1
+        tiles = 2 * E
+        scalar_copy = nc.scalar.copy
+        vector_copy = nc.vector.tensor_copy
+        gather(0)
+        layer1(0, 0)
+        gather(1)
+        layer1(0, 1)
+        gather(2)
+        ahead = 3
+        for t in range(tiles):
+            if t + 2 < tiles:
+                layer1((t + 2) // 2, (t + 2) % 2)
+            glu(t // 2, t % 2)
+            if ahead < len(runs) and runs[ahead][0] <= (t + 5) * P:
+                gather(ahead)
+                ahead += 1
+            if t > 1 and t % 2 == 0:
+                turn(t // 2 - 1, both, scalar_copy)
+            if t == tiles - 2:
+                turn(last, (0,), scalar_copy)
+            elif t > 3 and t % 2 == 0:
+                layer2(t // 2 - 2, both, psum_y, "y", scalar_copy)
+        turn(last, (1,), vector_copy)
+        layer2(last - 2, both, psum_y, "y", scalar_copy)
+        layer2(last - 1, both, psum_a, "a", scalar_copy)
+        layer2(last, (0,), psum_a, "a", scalar_copy)
+        layer2(last, (1,), psum_y, "y", vector_copy)
+
+        parts = [keep.tile([P, T], F32, name=f"part{r}") for r in range(TOP)]
+
+        def fetch(r):
+            nc.vector.tensor_tensor(parts[r][:], y_all[:].indirect(positions[r][:]), gates[:, r, :], MULT)
+
+        two = keep.tile([P, T], F32, name="two")
+        three = keep.tile([P, T], F32, name="three")
+        total = keep.tile([P, T], F32, name="total")
+        fetch(0)
+        fetch(1)
+        fetch(2)
+        nc.vector.tensor_tensor(two[:], parts[0][:], parts[1][:], ADD)
+        fetch(3)
+        pieces3 = (slice(0, 256), slice(256, 512))
+        for cols in pieces3:
+            nc.vector.tensor_tensor(three[:, cols], two[:, cols], parts[2][:, cols], ADD)
+        for cols in (slice(0, 256), slice(256, 384), slice(384, 512)):
+            nc.vector.tensor_tensor(total[:, cols], three[:, cols], parts[3][:, cols], ADD)
+            nc.sync.dma_start(out[:, cols], total[:, cols])

@@ -227,21 +227,45 @@ def tile_moe_tk_glu_silu_kernel(
         layer2(last, (1,), psum_y, "y", vector_copy)
 
         parts = [keep.tile([P, T], F32, name=f"part{r}") for r in range(TOP)]
-
-        def fetch(r):
-            nc.vector.tensor_tensor(parts[r][:], y_all[:].indirect(positions[r][:]), gates[:, r, :], MULT)
-
-        two = keep.tile([P, T], F32, name="two")
-        three = keep.tile([P, T], F32, name="three")
+        turned_sum = keep.tile([P, T], F32, name="turned_sum")
         total = keep.tile([P, T], F32, name="total")
-        fetch(0)
-        fetch(1)
-        fetch(2)
-        nc.vector.tensor_tensor(two[:], parts[0][:], parts[1][:], ADD)
-        fetch(3)
-        pieces3 = (slice(0, 256), slice(256, 512))
-        for cols in pieces3:
-            nc.vector.tensor_tensor(three[:, cols], two[:, cols], parts[2][:, cols], ADD)
-        for cols in (slice(0, 256), slice(256, 384), slice(384, 512)):
-            nc.vector.tensor_tensor(total[:, cols], three[:, cols], parts[3][:, cols], ADD)
+        halves = (slice(0, T // 2), slice(T // 2, T))
+        sums = [(psum_a, "a"), (psum_a, "a"), (psum_b, "b"), (psum_b, "b")]
+        sums = [pool.tile([P, P], F32, name=name) for pool, name in sums]
+
+        def fetch(r, cols):
+            mine = positions[r][:, cols.start // 16 : cols.stop // 16]
+            nc.vector.tensor_tensor(parts[r][:, cols], y_all[:].indirect(mine), gates[:, r, cols], MULT)
+
+        def add_turned(r, cols):
+            for b in range(cols.start // P, cols.stop // P):
+                nc.tensor.matmul(
+                    sums[b][:],
+                    parts[r][:, b * P : (b + 1) * P],
+                    ident[:],
+                    start=(r == 0),
+                    stop=(r == TOP - 2),
+                    is_transpose=True,
+                )
+
+        def turn_back(cols):
+            bank = psum_t.tile([P, T // 2], F32, name="bank")
+            for b in range(cols.start // P, cols.stop // P):
+                block = slice(b * P, (b + 1) * P)
+                nc.scalar.copy(turned_sum[:, block], sums[b][:])
+                nc.tensor.transpose(bank[:, b * P - cols.start : (b + 1) * P - cols.start], turned_sum[:, block], ident[:])
+            return bank
+
+        for r in range(TOP - 2):
+            fetch(r, slice(0, T))
+            add_turned(r, slice(0, T))
+        banks = []
+        for cols in halves:
+            fetch(TOP - 2, cols)
+            add_turned(TOP - 2, cols)
+            banks.append(turn_back(cols))
+        for cols in halves:
+            fetch(TOP - 1, cols)
+        for cols, bank in zip(halves, banks):
+            nc.vector.tensor_tensor(total[:, cols], bank[:], parts[TOP - 1][:, cols], ADD)
             nc.sync.dma_start(out[:, cols], total[:, cols])

@@ -27,10 +27,9 @@ def tile_moe_tk_glu_silu_kernel(
     nc = tc.nc
     with ExitStack() as ctx:
         keep = ctx.enter_context(tc.tile_pool(name="keep", bufs=1))
-        flow = ctx.enter_context(tc.tile_pool(name="flow", bufs=4))
-        psum_a = ctx.enter_context(tc.psum_pool(name="psum_a", bufs=2))
+        flow = ctx.enter_context(tc.tile_pool(name="flow", bufs=6))
+        psum_a = ctx.enter_context(tc.psum_pool(name="psum_a", bufs=1))
         psum_b = ctx.enter_context(tc.psum_pool(name="psum_b", bufs=3))
-        psum_t = ctx.enter_context(tc.psum_pool(name="psum_t", bufs=2))
         psum_y = ctx.enter_context(tc.psum_pool(name="psum_y", bufs=1))
 
         offsets = keep.tile([P, S // 16], U16, name="offsets")
@@ -111,16 +110,18 @@ def tile_moe_tk_glu_silu_kernel(
         quantise(384, 512)
 
         gathered = {}
-        runs = [(0, 128), (128, 512), (512, 896), (896, 1280), (1280, 1664), (1664, 2048)]
+        runs = [(0, P), (P, 2 * C)] + [(e * C, (e + 1) * C) for e in range(2, E)]
         first = {}
         hidden = {}
         turned = {}
-        on_gpsimd = ()
+        second = {}
+        gated = {}
 
         def gather(g):
             lo, hi = runs[g]
-            codes = flow.tile([P, hi - lo], U32, name="codes", align_bytes=64)
-            scales = flow.tile([P, hi - lo], U8, name="scales", align_bytes=64)
+            tag = min(g, 2)
+            codes = keep.tile([P, hi - lo], U32, name=f"codes{tag}", align_bytes=64, bufs=2 if tag == 2 else 1)
+            scales = keep.tile([P, hi - lo], U8, name=f"scales{tag}", align_bytes=64, bufs=2 if tag == 2 else 1)
             mine = offsets[:, lo // 16 : hi // 16]
             nc.vector.tensor_copy(codes[:], x_codes[:].indirect(mine))
             nc.vector.tensor_copy(scales[:], x_scales[:].indirect(mine))
@@ -128,21 +129,18 @@ def tile_moe_tk_glu_silu_kernel(
                 cols = slice(t * P - lo, t * P - lo + P)
                 gathered[t] = (codes[:, cols], scales[:, cols])
 
-        def layer1(e, s):
-            codes, scales = gathered.pop(2 * e + s)
-            a = psum_a.tile([P, H], F32, name="a")
-            b = psum_b.tile([P, H], F32, name="b")
-            for bank, words, plane in ((a, words1, plane1), (b, words3, plane3)):
-                nc.tensor.matmul_mx(
-                    out=bank[:],
-                    lhsT=codes.bitcast(FP8X4),
-                    lhsT_scale=scales,
-                    rhs=words[e // 2][:, e % 2, :].bitcast(FP4X4),
-                    rhs_scale=plane[:, e, :],
-                    start=True,
-                    stop=True,
-                )
-            first[e, s] = (a, b)
+        def product(bank, t, words, plane):
+            e = t // 2
+            codes, scales = gathered[t]
+            nc.tensor.matmul_mx(
+                out=bank[:],
+                lhsT=codes.bitcast(FP8X4),
+                lhsT_scale=scales,
+                rhs=words[e // 2][:, e % 2, :].bitcast(FP4X4),
+                rhs_scale=plane[:, e, :],
+                start=True,
+                stop=True,
+            )
 
         def split(t):
             return t[:].rearrange("p (m u d) -> p u m d", u=2, d=2)
@@ -150,23 +148,26 @@ def tile_moe_tk_glu_silu_kernel(
         def pieces(t):
             return t[:].rearrange("p (u m d) -> p u m d", u=2, d=2)
 
-        def glu(e, s):
-            a, b = first.pop((e, s))
-            h = flow.tile([P, H], BF16, name="h", align_bytes=64)
+        def activate(t):
+            a = psum_a.tile([P, H], F32, name=f"shared{t % 4}")
+            product(a, t, words1, plane1)
             sa = flow.tile([P, H], F32, name="sa")
-            if (e, s) in on_gpsimd:
-                sb = flow.tile([P, H], F32, name="sb")
-                nc.scalar.copy(pieces(sb), split(b))
-                nc.scalar.activation(pieces(sa), split(a), SILU)
-                nc.gpsimd.tensor_tensor(h[:], sb[:], sa[:], MULT)
-            else:
-                nc.scalar.activation(pieces(sa), split(a), SILU)
-                nc.vector.tensor_tensor(pieces(h), split(b), pieces(sa), MULT)
-            hidden[e, s] = h
+            nc.scalar.activation(pieces(sa), split(a), SILU)
+            gated[t] = sa
 
-        def turn(e, tiles, copy):
+        def linear(t):
+            b = psum_b.tile([P, H], F32, name="b")
+            product(b, t, words3, plane3)
+            first[t] = b
+
+        def glu(t):
+            h = flow.tile([P, H], BF16, name="h", align_bytes=64)
+            nc.vector.tensor_tensor(pieces(h), split(first.pop(t)), pieces(gated.pop(t)), MULT)
+            hidden[t // 2, t % 2] = h
+
+        def turn(e, tiles, name, copy):
             n = len(tiles)
-            bank = psum_t.tile([P, n, 2, P], F32, name="bank")
+            bank = psum_a.tile([P, n, 2, P], F32, name=name)
             for i, s in enumerate(tiles):
                 h = hidden.pop((e, s))
                 for u in range(2):
@@ -177,7 +178,7 @@ def tile_moe_tk_glu_silu_kernel(
             )
             turned[e, tiles] = rows
 
-        def layer2(e, tiles, pool, name, copy):
+        def layer2(e, tiles, pool, name):
             rows = turned.pop((e, tiles))
             n = len(tiles) * P
             hc = flow.tile([P, n], U32, name="hc", align_bytes=64)
@@ -193,8 +194,11 @@ def tile_moe_tk_glu_silu_kernel(
                 start=True,
                 stop=True,
             )
+            second[e, tiles] = y
+
+        def collect(e, tiles, copy):
             lo = e * C + tiles[0] * P
-            copy(y_all[:, lo : lo + n], y[:])
+            copy(y_all[:, lo : lo + len(tiles) * P], second.pop((e, tiles))[:])
 
         both = (0, 1)
         last = E - 1
@@ -202,36 +206,45 @@ def tile_moe_tk_glu_silu_kernel(
         scalar_copy = nc.scalar.copy
         vector_copy = nc.vector.tensor_copy
         gather(0)
-        layer1(0, 0)
+        activate(0)
+        linear(0)
         gather(1)
-        layer1(0, 1)
+        for t in (1, 2):
+            activate(t)
+            linear(t)
+        activate(3)
         gather(2)
-        ahead = 3
         for t in range(tiles):
-            if t + 2 < tiles:
-                layer1((t + 2) // 2, (t + 2) % 2)
-            glu(t // 2, t % 2)
-            if ahead < len(runs) and runs[ahead][0] <= (t + 5) * P:
-                gather(ahead)
-                ahead += 1
-            if t > 1 and t % 2 == 0:
-                turn(t // 2 - 1, both, scalar_copy)
+            e = t // 2
+            glu(t)
+            if t + 3 < tiles:
+                linear(t + 3)
+            if t % 2 == 0 and 1 <= e < E - 2:
+                gather(e + 2)
+            if t + 4 < tiles:
+                activate(t + 4)
+            if t % 2 == 1 and e < last:
+                turn(e, both, f"shared{2 * e % 4}", scalar_copy)
+            if t % 2 == 1 and 1 <= e < last - 1:
+                layer2(e - 1, both, psum_a, f"shared{(2 * e + 1) % 4}")
+                collect(e - 1, both, scalar_copy)
             if t == tiles - 2:
-                turn(last, (0,), scalar_copy)
-            elif t > 3 and t % 2 == 0:
-                layer2(t // 2 - 2, both, psum_y, "y", scalar_copy)
-        turn(last, (1,), vector_copy)
-        layer2(last - 2, both, psum_y, "y", scalar_copy)
-        layer2(last - 1, both, psum_a, "a", scalar_copy)
-        layer2(last, (0,), psum_a, "a", scalar_copy)
-        layer2(last, (1,), psum_y, "y", vector_copy)
+                turn(last, (0,), "shared2", scalar_copy)
+        turn(last, (1,), "shared0", vector_copy)
+        for e, part, pool, name, copy in (
+            (last - 2, both, psum_y, "y", scalar_copy),
+            (last - 1, both, psum_a, "shared1", scalar_copy),
+            (last, (0,), psum_a, "shared3", scalar_copy),
+            (last, (1,), psum_y, "y", vector_copy),
+        ):
+            layer2(e, part, pool, name)
+            collect(e, part, copy)
 
         parts = [keep.tile([P, T], F32, name=f"part{r}") for r in range(TOP)]
         turned_sum = keep.tile([P, T], F32, name="turned_sum")
         total = keep.tile([P, T], F32, name="total")
         halves = (slice(0, T // 2), slice(T // 2, T))
-        sums = [(psum_a, "a"), (psum_a, "a"), (psum_b, "b"), (psum_b, "b")]
-        sums = [pool.tile([P, P], F32, name=name) for pool, name in sums]
+        sums = [psum_a.tile([P, P], F32, name=f"shared{b}") for b in range(T // P)]
 
         def fetch(r, cols):
             mine = positions[r][:, cols.start // 16 : cols.stop // 16]
@@ -249,7 +262,7 @@ def tile_moe_tk_glu_silu_kernel(
                 )
 
         def turn_back(cols):
-            bank = psum_t.tile([P, T // 2], F32, name="bank")
+            bank = psum_b.tile([P, T // 2], F32, name="b")
             for b in range(cols.start // P, cols.stop // P):
                 block = slice(b * P, (b + 1) * P)
                 nc.scalar.copy(turned_sum[:, block], sums[b][:])

@@ -27,17 +27,17 @@ def tile_moe_tk_glu_silu_kernel(
     nc = tc.nc
     with ExitStack() as ctx:
         keep = ctx.enter_context(tc.tile_pool(name="keep", bufs=1))
-        flow = ctx.enter_context(tc.tile_pool(name="flow", bufs=6))
+        flow = ctx.enter_context(tc.tile_pool(name="flow", bufs=4))
+        wide = ctx.enter_context(tc.tile_pool(name="wide", bufs=2 * E))
         psum_a = ctx.enter_context(tc.psum_pool(name="psum_a", bufs=1))
-        psum_b = ctx.enter_context(tc.psum_pool(name="psum_b", bufs=3))
-        psum_y = ctx.enter_context(tc.psum_pool(name="psum_y", bufs=1))
+        psum_b = ctx.enter_context(tc.psum_pool(name="psum_b", bufs=4))
 
         offsets = keep.tile([P, S // 16], U16, name="offsets")
         positions = [keep.tile([P, T // 16], U16, name=f"positions{r}") for r in range(TOP)]
         x_raw = keep.tile([P, 4, T], F32, name="x_raw")
         x_rows = keep.tile([P, T, 4], BF16, name="x_rows", align_bytes=64)
-        x_codes = keep.tile([P, T], U32, name="x_codes", align_bytes=64)
-        x_scales = keep.tile([P, T], U8, name="x_scales", align_bytes=64)
+        x_codes = keep.tile([P, 2 * T], U32, name="x_codes", align_bytes=64)
+        x_scales = keep.tile([P, 2 * T], U8, name="x_scales", align_bytes=64)
         gates = keep.tile([P, TOP, T], F32, name="gates")
         y_all = keep.tile([P, S], F32, name="y_all")
         ident = keep.tile([P, P], F32, name="ident")
@@ -73,6 +73,7 @@ def tile_moe_tk_glu_silu_kernel(
         zero(plane3)
         zero(plane2)
         nc.gpsimd.memset(x_scales[:], 0)
+        nc.gpsimd.memset(x_codes[:, T:], 0)
         make_identity(nc, ident[:])
         load_plane(plane1, w1_scales, 0, E)
         load_words(words1[0], w1_words, 0, 2)
@@ -110,18 +111,18 @@ def tile_moe_tk_glu_silu_kernel(
         quantise(384, 512)
 
         gathered = {}
-        runs = [(0, P), (P, 2 * C)] + [(e * C, (e + 1) * C) for e in range(2, E)]
+        runs = [[0,128],[128,512],[512,1280],[1280,2048]]
         first = {}
         hidden = {}
         turned = {}
         second = {}
         gated = {}
+        pooled = 4
 
         def gather(g):
             lo, hi = runs[g]
-            tag = min(g, 2)
-            codes = keep.tile([P, hi - lo], U32, name=f"codes{tag}", align_bytes=64, bufs=2 if tag == 2 else 1)
-            scales = keep.tile([P, hi - lo], U8, name=f"scales{tag}", align_bytes=64, bufs=2 if tag == 2 else 1)
+            codes = keep.tile([P, hi - lo], U32, name=f"codes{g}", align_bytes=64)
+            scales = keep.tile([P, hi - lo], U8, name=f"scales{g}", align_bytes=64)
             mine = offsets[:, lo // 16 : hi // 16]
             nc.vector.tensor_copy(codes[:], x_codes[:].indirect(mine))
             nc.vector.tensor_copy(scales[:], x_scales[:].indirect(mine))
@@ -149,102 +150,98 @@ def tile_moe_tk_glu_silu_kernel(
             return t[:].rearrange("p (u m d) -> p u m d", u=2, d=2)
 
         def activate(t):
-            a = psum_a.tile([P, H], F32, name=f"shared{t % 4}")
+            a = psum_a.tile([P, H], F32, name=f"a{t % 4}")
             product(a, t, words1, plane1)
-            sa = flow.tile([P, H], F32, name="sa")
+            if t == pooled:
+                sa = keep.tile([P, H], F32, name="after_first_product", align_bytes=64)
+            else:
+                sa = wide.tile([P, H], F32, name="sa")
             nc.scalar.activation(pieces(sa), split(a), SILU)
             gated[t] = sa
 
         def linear(t):
             b = psum_b.tile([P, H], F32, name="b")
             product(b, t, words3, plane3)
+            if t < pooled:
+                if t == pooled - 1:
+                    sb = keep.tile([P, H], F32, name="after_gpsimd", align_bytes=64)
+                else:
+                    sb = wide.tile([P, H], F32, name="sb")
+                nc.scalar.copy(pieces(sb), split(b))
+                b = sb
             first[t] = b
 
         def glu(t):
-            h = flow.tile([P, H], BF16, name="h", align_bytes=64)
+            h = wide.tile([P, H], BF16, name="h", align_bytes=64)
             nc.vector.tensor_tensor(pieces(h), split(first.pop(t)), pieces(gated.pop(t)), MULT)
-            hidden[t // 2, t % 2] = h
+            hidden[t] = h[:]
 
-        def turn(e, tiles, name, copy):
-            n = len(tiles)
-            bank = psum_a.tile([P, n, 2, P], F32, name=name)
-            for i, s in enumerate(tiles):
-                h = hidden.pop((e, s))
+        def turn(e, pool, name, copy):
+            bank = pool.tile([P, 2, 2, P], F32, name=name)
+            for s in range(2):
+                h = hidden.pop(2 * e + s)
                 for u in range(2):
-                    nc.tensor.transpose(bank[:, i, u, :], h[:, u * 256 : (u + 1) * 256].bitcast(F32), ident[:])
-            rows = flow.tile([P, n * P * 4], BF16, name="rows", align_bytes=64)
+                    nc.tensor.transpose(bank[:, s, u, :], h[:, u * 256 : (u + 1) * 256].bitcast(F32), ident[:])
+            rows = wide.tile([P, C * 4], BF16, name="rows", align_bytes=64)
             copy(
-                rows[:].bitcast(F32).rearrange("p (s c u) -> p s c u", s=n, u=2), bank[:].rearrange("p s u c -> p s c u")
+                rows[:].bitcast(F32).rearrange("p (s c u) -> p s c u", s=2, u=2), bank[:].rearrange("p s u c -> p s c u")
             )
-            turned[e, tiles] = rows
+            turned[e] = rows
 
-        def layer2(e, tiles, pool, name):
-            rows = turned.pop((e, tiles))
-            n = len(tiles) * P
-            hc = flow.tile([P, n], U32, name="hc", align_bytes=64)
-            hs = flow.tile([P, n], U8, name="hs", align_bytes=64)
-            nc.vector.quantize_mx(out=hc[:].bitcast(FP8X4), scales=hs[:], in_=rows[:])
-            y = pool.tile([P, n], F32, name=name)
+        def layer2(e, pool, name, copy):
+            mine = slice(e * C, (e + 1) * C)
+            nc.vector.quantize_mx(out=h_codes[:, mine].bitcast(FP8X4), scales=h_scales[:, mine], in_=turned.pop(e)[:])
+            y = pool.tile([P, C], F32, name=name)
             nc.tensor.matmul_mx(
                 out=y[:],
                 lhsT=words2[:, e, :].bitcast(FP4X4),
                 lhsT_scale=plane2[:, e, :],
-                rhs=hc[:].bitcast(FP8X4),
-                rhs_scale=hs[:],
+                rhs=h_codes[:, mine].bitcast(FP8X4),
+                rhs_scale=h_scales[:, mine],
                 start=True,
                 stop=True,
             )
-            second[e, tiles] = y
+            copy(y_all[:, mine], y[:])
 
-        def collect(e, tiles, copy):
-            lo = e * C + tiles[0] * P
-            copy(y_all[:, lo : lo + len(tiles) * P], second.pop((e, tiles))[:])
-
-        both = (0, 1)
-        last = E - 1
         tiles = 2 * E
         scalar_copy = nc.scalar.copy
         vector_copy = nc.vector.tensor_copy
-        gather(0)
-        activate(0)
-        linear(0)
-        gather(1)
-        for t in (1, 2):
+        for g in range(len(runs)):
+            gather(g)
+        for t in range(tiles):
             activate(t)
             linear(t)
-        activate(3)
-        gather(2)
-        for t in range(tiles):
-            e = t // 2
-            glu(t)
-            if t + 3 < tiles:
-                linear(t + 3)
-            if t % 2 == 0 and 1 <= e < E - 2:
-                gather(e + 2)
-            if t + 4 < tiles:
-                activate(t + 4)
-            if t % 2 == 1 and e < last:
-                turn(e, both, f"shared{2 * e % 4}", scalar_copy)
-            if t % 2 == 1 and 1 <= e < last - 1:
-                layer2(e - 1, both, psum_a, f"shared{(2 * e + 1) % 4}")
-                collect(e - 1, both, scalar_copy)
-            if t == tiles - 2:
-                turn(last, (0,), "shared2", scalar_copy)
-        turn(last, (1,), "shared0", vector_copy)
-        for e, part, pool, name, copy in (
-            (last - 2, both, psum_y, "y", scalar_copy),
-            (last - 1, both, psum_a, "shared1", scalar_copy),
-            (last, (0,), psum_a, "shared3", scalar_copy),
-            (last, (1,), psum_y, "y", vector_copy),
-        ):
-            layer2(e, part, pool, name)
-            collect(e, part, copy)
+            if t >= pooled:
+                glu(t)
+            if t == pooled:
+                h_pooled = keep.tile([P, pooled, H], BF16, name="after_first_product", align_bytes=64)
+                for i in range(pooled):
+                    nc.gpsimd.tensor_tensor(h_pooled[:, i, :], first.pop(i)[:], gated.pop(i)[:], MULT)
+                    hidden[i] = h_pooled[:, i, :]
+        h_codes = keep.tile([P, S], U32, name="after_gpsimd", align_bytes=64)
+        h_scales = keep.tile([P, S], U8, name="h_scales", align_bytes=64)
+        turn(2, psum_a, "a0", scalar_copy)
+        turn(3, psum_a, "a1", scalar_copy)
+        turn(0, psum_a, "a2", scalar_copy)
+        turn(4, psum_b, "b", scalar_copy)
+        turn(1, psum_a, "a3", scalar_copy)
+        turn(5, psum_b, "b", scalar_copy)
+        layer2(2, psum_a, "a0", scalar_copy)
+        layer2(3, psum_a, "a1", scalar_copy)
+        turn(6, psum_b, "b", vector_copy)
+        layer2(0, psum_a, "a2", scalar_copy)
+        layer2(4, psum_a, "a3", scalar_copy)
+        turn(7, psum_b, "b", vector_copy)
+        layer2(1, psum_a, "a0", scalar_copy)
+        layer2(5, psum_a, "a1", scalar_copy)
+        layer2(6, psum_a, "a2", scalar_copy)
+        layer2(7, psum_a, "a3", vector_copy)
 
         parts = [keep.tile([P, T], F32, name=f"part{r}") for r in range(TOP)]
         turned_sum = keep.tile([P, T], F32, name="turned_sum")
         total = keep.tile([P, T], F32, name="total")
         halves = (slice(0, T // 2), slice(T // 2, T))
-        sums = [psum_a.tile([P, P], F32, name=f"shared{b}") for b in range(T // P)]
+        sums = [psum_a.tile([P, P], F32, name=f"a{b}") for b in range(T // P)]
 
         def fetch(r, cols):
             mine = positions[r][:, cols.start // 16 : cols.stop // 16]

@@ -29,8 +29,7 @@ def tile_moe_tk_glu_silu_kernel(
         keep = ctx.enter_context(tc.tile_pool(name="keep", bufs=1))
         flow = ctx.enter_context(tc.tile_pool(name="flow", bufs=4))
         wide = ctx.enter_context(tc.tile_pool(name="wide", bufs=2 * E))
-        psum_a = ctx.enter_context(tc.psum_pool(name="psum_a", bufs=1))
-        psum_b = ctx.enter_context(tc.psum_pool(name="psum_b", bufs=4))
+        psum = ctx.enter_context(tc.psum_pool(name="psum", bufs=1))
 
         offsets = keep.tile([P, S // 16], U16, name="offsets")
         positions = [keep.tile([P, T // 16], U16, name=f"positions{r}") for r in range(TOP)]
@@ -46,7 +45,9 @@ def tile_moe_tk_glu_silu_kernel(
         plane1 = keep.tile([P, E, H], U8, name="plane1", align_bytes=64)
         plane3 = keep.tile([P, E, H], U8, name="plane3", align_bytes=64)
         plane2 = keep.tile([P, E, N], U8, name="plane2", align_bytes=64)
-        words1 = [keep.tile([P, 2, 2 * H], U8, name=f"words1_{i}", align_bytes=64) for i in range(E // 2)]
+        words1 = {i: keep.tile([P, 2, 2 * H], U8, name=f"words1_{i}", align_bytes=64) for i in (0, 1, 3)}
+        words1[2] = keep.tile([P, 1, 2 * H], U8, name="after_w1_of_tile_9", align_bytes=64)
+        words1_5 = keep.tile([P, 1, 2 * H], U8, name="words1_5", align_bytes=64)
         words3 = [keep.tile([P, 2, 2 * H], U8, name=f"words3_{i}", align_bytes=64) for i in range(E // 2)]
         words2 = keep.tile([P, E, 2 * N], U8, name="words2", align_bytes=64)
 
@@ -81,11 +82,13 @@ def tile_moe_tk_glu_silu_kernel(
         load_plane(plane3, w3_scales, 0, E)
         load_words(words1[1], w1_words, 2, 4)
         load_words(words3[1], w3_words, 2, 4)
+        load_words(words1[2], w1_words, 4, 5)
+        load_words(words1_5, w1_words, 5, 6)
+        load_words(words3[2], w3_words, 4, 6)
+        load_words(words1[3], w1_words, 6, 8)
+        load_words(words3[3], w3_words, 6, 8)
         load_plane(plane2, w2_scales, 0, E)
         load_words(words2, w2_words, 0, E)
-        for i in range(2, E // 2):
-            load_words(words1[i], w1_words, 2 * i, 2 * i + 2)
-            load_words(words3[i], w3_words, 2 * i, 2 * i + 2)
         for tile, pos in zip(positions, (pos1, pos2, pos3, pos4)):
             nc.sync.dma_start(tile[:], pos)
         nc.sync.dma_start(gates[:], gate.rearrange("r p t -> p r t"))
@@ -111,13 +114,13 @@ def tile_moe_tk_glu_silu_kernel(
         quantise(384, 512)
 
         gathered = {}
-        runs = [[0,128],[128,512],[512,1280],[1280,2048]]
+        runs = [[0,256],[256,512],[512,1024],[1024,1536],[1536,2048]]
         first = {}
         hidden = {}
         turned = {}
         second = {}
         gated = {}
-        pooled = 4
+        pooled = 5
 
         def gather(g):
             lo, hi = runs[g]
@@ -133,11 +136,15 @@ def tile_moe_tk_glu_silu_kernel(
         def product(bank, t, words, plane):
             e = t // 2
             codes, scales = gathered[t]
+            if e == 5 and words is words1:
+                moving = words1_5[:, 0, :]
+            else:
+                moving = words[e // 2][:, e % 2, :]
             nc.tensor.matmul_mx(
                 out=bank[:],
                 lhsT=codes.bitcast(FP8X4),
                 lhsT_scale=scales,
-                rhs=words[e // 2][:, e % 2, :].bitcast(FP4X4),
+                rhs=moving.bitcast(FP4X4),
                 rhs_scale=plane[:, e, :],
                 start=True,
                 stop=True,
@@ -149,18 +156,18 @@ def tile_moe_tk_glu_silu_kernel(
         def pieces(t):
             return t[:].rearrange("p (u m d) -> p u m d", u=2, d=2)
 
-        def activate(t):
-            a = psum_a.tile([P, H], F32, name=f"a{t % 4}")
+        def activate(t, bank):
+            a = psum.tile([P, H], F32, name=f"bank{bank}")
             product(a, t, words1, plane1)
-            if t == pooled:
-                sa = keep.tile([P, H], F32, name="after_first_product", align_bytes=64)
+            if t == 2 * E - 1:
+                sa = keep.tile([P, H], F32, name="after_last_product", align_bytes=64)
             else:
                 sa = wide.tile([P, H], F32, name="sa")
             nc.scalar.activation(pieces(sa), split(a), SILU)
             gated[t] = sa
 
-        def linear(t):
-            b = psum_b.tile([P, H], F32, name="b")
+        def linear(t, bank):
+            b = psum.tile([P, H], F32, name=f"bank{bank}")
             product(b, t, words3, plane3)
             if t < pooled:
                 if t == pooled - 1:
@@ -172,12 +179,12 @@ def tile_moe_tk_glu_silu_kernel(
             first[t] = b
 
         def glu(t):
-            h = wide.tile([P, H], BF16, name="h", align_bytes=64)
+            h = h_all[:, t - pooled, :]
             nc.vector.tensor_tensor(pieces(h), split(first.pop(t)), pieces(gated.pop(t)), MULT)
-            hidden[t] = h[:]
+            hidden[t] = h
 
-        def turn(e, pool, name, copy):
-            bank = pool.tile([P, 2, 2, P], F32, name=name)
+        def turn(e, number, copy):
+            bank = psum.tile([P, 2, 2, P], F32, name=f"bank{number}")
             for s in range(2):
                 h = hidden.pop(2 * e + s)
                 for u in range(2):
@@ -188,10 +195,10 @@ def tile_moe_tk_glu_silu_kernel(
             )
             turned[e] = rows
 
-        def layer2(e, pool, name, copy):
+        def layer2(e, bank):
             mine = slice(e * C, (e + 1) * C)
             nc.vector.quantize_mx(out=h_codes[:, mine].bitcast(FP8X4), scales=h_scales[:, mine], in_=turned.pop(e)[:])
-            y = pool.tile([P, C], F32, name=name)
+            y = psum.tile([P, C], F32, name=f"bank{bank}")
             nc.tensor.matmul_mx(
                 out=y[:],
                 lhsT=words2[:, e, :].bitcast(FP4X4),
@@ -201,47 +208,66 @@ def tile_moe_tk_glu_silu_kernel(
                 start=True,
                 stop=True,
             )
-            copy(y_all[:, mine], y[:])
+            second[e] = y
+
+        def collect(e, copy):
+            copy(y_all[:, e * C : (e + 1) * C], second.pop(e)[:])
 
         tiles = 2 * E
         scalar_copy = nc.scalar.copy
         vector_copy = nc.vector.tensor_copy
         for g in range(len(runs)):
             gather(g)
-        for t in range(tiles):
-            activate(t)
-            linear(t)
-            if t >= pooled:
-                glu(t)
+        for pair in range(2):
+            for i in range(2):
+                activate(2 * pair + i, 4 * pair + i)
+            for i in range(2):
+                linear(2 * pair + i, 4 * pair + 2 + i)
+        activate(4, 0)
+        linear(4, 1)
+        for t in range(5, 8):
+            activate(t, t - 3)
+        for t in range(5, 8):
+            linear(t, t)
+        activate(8, 0)
+        linear(8, 1)
+        for t in range(9, 12):
+            activate(t, t - 7)
+        h_all = keep.tile([P, tiles - pooled, H], BF16, name="after_w1_of_tile_9", align_bytes=64)
+        a_banks = {12: 5, 13: 6, 14: 7, 15: 1}
+        b_banks = {9: 0, 10: 2, 11: 3, 12: 4, 13: 0, 14: 2, 15: 3}
+        for t in range(pooled, tiles):
+            if t in b_banks:
+                linear(t, b_banks[t])
+            glu(t)
+            if t + 7 < tiles:
+                activate(t + 7, a_banks[t + 7])
             if t == pooled:
-                h_pooled = keep.tile([P, pooled, H], BF16, name="after_first_product", align_bytes=64)
+                h_pooled = keep.tile([P, pooled, H], BF16, name="x_scales", align_bytes=64)
                 for i in range(pooled):
                     nc.gpsimd.tensor_tensor(h_pooled[:, i, :], first.pop(i)[:], gated.pop(i)[:], MULT)
                     hidden[i] = h_pooled[:, i, :]
         h_codes = keep.tile([P, S], U32, name="after_gpsimd", align_bytes=64)
-        h_scales = keep.tile([P, S], U8, name="h_scales", align_bytes=64)
-        turn(2, psum_a, "a0", scalar_copy)
-        turn(3, psum_a, "a1", scalar_copy)
-        turn(0, psum_a, "a2", scalar_copy)
-        turn(4, psum_b, "b", scalar_copy)
-        turn(1, psum_a, "a3", scalar_copy)
-        turn(5, psum_b, "b", scalar_copy)
-        layer2(2, psum_a, "a0", scalar_copy)
-        layer2(3, psum_a, "a1", scalar_copy)
-        turn(6, psum_b, "b", vector_copy)
-        layer2(0, psum_a, "a2", scalar_copy)
-        layer2(4, psum_a, "a3", scalar_copy)
-        turn(7, psum_b, "b", vector_copy)
-        layer2(1, psum_a, "a0", scalar_copy)
-        layer2(5, psum_a, "a1", scalar_copy)
-        layer2(6, psum_a, "a2", scalar_copy)
-        layer2(7, psum_a, "a3", vector_copy)
+        h_scales = keep.tile([P, S], U8, name="after_last_product", align_bytes=64)
+        for e, bank in ((3, 5), (0, 6)):
+            turn(e, bank, scalar_copy)
+        turn(5, 4, vector_copy)
+        for e, bank in ((4, 7), (1, 1)):
+            turn(e, bank, scalar_copy)
+        for e, bank in ((6, 0), (2, 2), (7, 3)):
+            turn(e, bank, scalar_copy)
+        for e, bank in ((3, 5), (0, 6), (4, 7), (5, 4), (1, 1), (6, 0), (2, 2), (7, 3)):
+            layer2(e, bank)
+        for e in (3, 0, 4, 5, 1):
+            collect(e, scalar_copy)
+        for e in (6, 2, 7):
+            collect(e, vector_copy)
 
         parts = [keep.tile([P, T], F32, name=f"part{r}") for r in range(TOP)]
         turned_sum = keep.tile([P, T], F32, name="turned_sum")
         total = keep.tile([P, T], F32, name="total")
         halves = (slice(0, T // 2), slice(T // 2, T))
-        sums = [psum_a.tile([P, P], F32, name=f"a{b}") for b in range(T // P)]
+        sums = [psum.tile([P, P], F32, name=f"bank{b}") for b in range(T // P)]
 
         def fetch(r, cols):
             mine = positions[r][:, cols.start // 16 : cols.stop // 16]
@@ -259,7 +285,7 @@ def tile_moe_tk_glu_silu_kernel(
                 )
 
         def turn_back(cols):
-            bank = psum_b.tile([P, T // 2], F32, name="b")
+            bank = psum.tile([P, T // 2], F32, name=f"bank{4 + cols.start // (T // 2)}")
             for b in range(cols.start // P, cols.stop // P):
                 block = slice(b * P, (b + 1) * P)
                 nc.scalar.copy(turned_sum[:, block], sums[b][:])

@@ -243,7 +243,7 @@ def tile_moe_tk_glu_silu_kernel(
             if t + 7 < tiles:
                 activate(t + 7, a_banks[t + 7])
             if t == pooled:
-                h_pooled = keep.tile([P, pooled, H], BF16, name="x_scales", align_bytes=64)
+                h_pooled = keep.tile([P, pooled, H], BF16, name="h_pooled", align_bytes=64)
                 for i in range(pooled):
                     nc.gpsimd.tensor_tensor(h_pooled[:, i, :], first.pop(i)[:], gated.pop(i)[:], MULT)
                     hidden[i] = h_pooled[:, i, :]

@@ -8,6 +8,13 @@ P = 128
 S = E * C
 FLOPS = 2 * S * (2 * K * H + H * N)
 
+TURNED = 4
+DIRECT = E - TURNED
+POOLED = 3
+BLOCKS = K // 32
+RUNS = ((0, 256), (256, 512), (512, 1024), (1024, 1536), (1536, 2048))
+PLACES = (4, 5, 0, 6, 3, 7, 1, 2)
+
 F32 = mybir.dt.float32
 BF16 = mybir.dt.bfloat16
 I32 = mybir.dt.int32
@@ -27,8 +34,6 @@ def tile_moe_tk_glu_silu_kernel(
     nc = tc.nc
     with ExitStack() as ctx:
         keep = ctx.enter_context(tc.tile_pool(name="keep", bufs=1))
-        flow = ctx.enter_context(tc.tile_pool(name="flow", bufs=4))
-        wide = ctx.enter_context(tc.tile_pool(name="wide", bufs=2 * E))
         psum = ctx.enter_context(tc.psum_pool(name="psum", bufs=1))
 
         offsets = keep.tile([P, S // 16], U16, name="offsets")
@@ -37,58 +42,92 @@ def tile_moe_tk_glu_silu_kernel(
         x_rows = keep.tile([P, T, 4], BF16, name="x_rows", align_bytes=64)
         x_codes = keep.tile([P, 2 * T], U32, name="x_codes", align_bytes=64)
         x_scales = keep.tile([P, 2 * T], U8, name="x_scales", align_bytes=64)
-        gates = keep.tile([P, TOP, T], F32, name="gates")
-        y_all = keep.tile([P, S], F32, name="y_all")
         ident = keep.tile([P, P], F32, name="ident")
         one = keep.tile([P, 1], F32, name="one")
 
-        plane1 = keep.tile([P, E, H], U8, name="plane1", align_bytes=64)
-        plane3 = keep.tile([P, E, H], U8, name="plane3", align_bytes=64)
-        plane2 = keep.tile([P, E, N], U8, name="plane2", align_bytes=64)
-        words1 = {i: keep.tile([P, 2, 2 * H], U8, name=f"words1_{i}", align_bytes=64) for i in (0, 1, 3)}
-        words1[2] = keep.tile([P, 1, 2 * H], U8, name="after_w1_of_tile_9", align_bytes=64)
-        words1_5 = keep.tile([P, 1, 2 * H], U8, name="words1_5", align_bytes=64)
-        words3 = [keep.tile([P, 2, 2 * H], U8, name=f"words3_{i}", align_bytes=64) for i in range(E // 2)]
+        plane1 = keep.tile([P, TURNED, H], U8, name="plane1", align_bytes=64)
+        plane3 = keep.tile([P, TURNED, H], U8, name="plane3", align_bytes=64)
+        spread = keep.tile([P, H], U8, name="spread", align_bytes=64)
+        spread_moved = keep.tile([P, H], U8, name="spread_moved", align_bytes=64)
+        moved_plane1 = keep.tile([P, DIRECT, H], U8, name="moved_plane1", align_bytes=64)
+        moved_plane3 = keep.tile([P, DIRECT, H], U8, name="moved_plane3", align_bytes=64)
+        pairs1 = {lo: keep.tile([P, 2, 2 * H], U8, name=f"words1_{lo}", align_bytes=64) for lo in (0, 2, 4)}
+        pairs3 = {lo: keep.tile([P, 2, 2 * H], U8, name=f"words3_{lo}", align_bytes=64) for lo in (0, 2, 4)}
+        late_words = keep.tile([P, 4, 2 * H], U8, name="late_words", align_bytes=64)
         words2 = keep.tile([P, E, 2 * N], U8, name="words2", align_bytes=64)
 
-        def zero(plane):
-            nc.vector.memset(plane[:].rearrange("p e i -> p (e i)").bitcast(I32), 0)
+        def as_words(plane):
+            return plane[:].rearrange("p e i -> p (e i)").bitcast(I32)
 
-        def load_plane(plane, scales, lo, hi):
+        def load_plane(plane, scales, experts):
             rows = scales.bitcast(I32).rearrange("e s (q r) i -> r q (e s) i", r=4)
             for r in range(4):
-                nc.sync.dma_start(plane[r:P:32, :, :].bitcast(I32), rows[r][:, lo:hi, :])
+                nc.sync.dma_start(plane[r:P:32, :, :].bitcast(I32), rows[r][:, :experts, :])
 
         def load_words(tile, words, lo, hi):
-            nc.sync.dma_start(tile[:].bitcast(I32), words.bitcast(I32).rearrange("e s p i -> p (e s) i")[:, lo:hi, :])
+            nc.sync.dma_start(tile.bitcast(I32), words.bitcast(I32).rearrange("e s p i -> p (e s) i")[:, lo:hi, :])
 
         x_view = xT.rearrange("(p j) t -> p j t", j=4)
-        half = T // 2
-        for i in range(2):
-            cols = slice(i * half, (i + 1) * half)
-            nc.sync.dma_start(x_raw[:, :, cols], x_view[:, :, cols])
+        for lo in (0, T // 2):
+            nc.sync.dma_start(x_raw[:, :, lo : lo + T // 2], x_view[:, :, lo : lo + T // 2])
         nc.sync.dma_start(offsets[:], offs)
         nc.vector.memset(one[:], 0.0)
         nc.scalar.activation(one[:], one[:], SILU)
-        zero(plane1)
-        zero(plane3)
-        zero(plane2)
+        for plane in (plane1, plane3, moved_plane1, moved_plane3):
+            nc.vector.memset(as_words(plane), 0)
         nc.gpsimd.memset(x_scales[:], 0)
         nc.gpsimd.memset(x_codes[:, T:], 0)
         make_identity(nc, ident[:])
-        load_plane(plane1, w1_scales, 0, E)
-        load_words(words1[0], w1_words, 0, 2)
-        load_words(words3[0], w3_words, 0, 2)
-        load_plane(plane3, w3_scales, 0, E)
-        load_words(words1[1], w1_words, 2, 4)
-        load_words(words3[1], w3_words, 2, 4)
-        load_words(words1[2], w1_words, 4, 5)
-        load_words(words1_5, w1_words, 5, 6)
-        load_words(words3[2], w3_words, 4, 6)
-        load_words(words1[3], w1_words, 6, 8)
-        load_words(words3[3], w3_words, 6, 8)
-        load_plane(plane2, w2_scales, 0, E)
-        load_words(words2, w2_words, 0, E)
+
+        first1, first3 = 0, BLOCKS * DIRECT
+
+        def load_spread(scales, first):
+            rows = scales.bitcast(I32).rearrange("e s q i -> q (e s) i")[:, TURNED:, :]
+            nc.sync.dma_start(spread[first : first + BLOCKS * DIRECT, :].bitcast(I32), rows)
+
+        def place(plane, first, quadrant):
+            start = first + quadrant * 4 * DIRECT
+            nc.sync.dma_start(
+                plane[32 * quadrant : 32 * quadrant + 4, :, :].bitcast(I32),
+                spread_moved[start : start + 4 * DIRECT, :].bitcast(I32),
+            )
+
+        moved = {}
+
+        def permute(source, keys):
+            fresh = keep.tile([P, len(keys), 2 * H], U8, name="moved_%s%d" % keys[0], align_bytes=64)
+            nc.gpsimd.tensor_copy(
+                fresh[:].bitcast(U16).rearrange("p e (j m) -> p e j m", j=4),
+                source[:].bitcast(U16).rearrange("p e (m j) -> p e j m", j=4),
+            )
+            for i, key in enumerate(keys):
+                moved[key] = fresh[:, i, :]
+
+        load_plane(plane1, w1_scales, TURNED)
+        load_words(pairs1[0][:], w1_words, 0, 2)
+        load_words(pairs1[4][:], w1_words, 4, 6)
+        load_spread(w1_scales, first1)
+        load_spread(w3_scales, first3)
+        load_plane(plane3, w3_scales, TURNED)
+        load_words(pairs3[0][:], w3_words, 0, 2)
+        load_words(pairs3[4][:], w3_words, 4, 6)
+        load_words(pairs3[2][:], w3_words, 2, 4)
+        load_words(pairs1[2][:], w1_words, 2, 4)
+        load_words(late_words[:, 0:2, :], w1_words, 6, 8)
+        load_words(late_words[:, 2:4, :], w3_words, 6, 8)
+        permute(pairs1[4], (("a", 4), ("a", 5)))
+        nc.gpsimd.tensor_copy(
+            spread_moved[:].rearrange("p (j m) -> p j m", j=4), spread[:].rearrange("p (m j) -> p j m", j=4)
+        )
+        for quadrant in range(4):
+            place(moved_plane3, first3, quadrant)
+            place(moved_plane1, first1, quadrant)
+        permute(pairs3[4], (("b", 4), ("b", 5)))
+        plane2 = keep.tile([P, E, N], U8, name="spread", align_bytes=64)
+        gates = keep.tile([P, TOP, T], F32, name="spread_moved", align_bytes=64)
+        nc.gpsimd.memset(as_words(plane2), 0)
+        load_plane(plane2, w2_scales, E)
+        load_words(words2[:], w2_words, 0, E)
         for tile, pos in zip(positions, (pos1, pos2, pos3, pos4)):
             nc.sync.dma_start(tile[:], pos)
         nc.sync.dma_start(gates[:], gate.rearrange("r p t -> p r t"))
@@ -96,7 +135,7 @@ def tile_moe_tk_glu_silu_kernel(
         def interleave(copy, lo, hi):
             copy(x_rows[:, lo:hi, :], x_raw[:, :, lo:hi].rearrange("p j t -> p t j"))
 
-        def quantise(lo, hi):
+        def quantise_tokens(lo, hi):
             nc.vector.quantize_mx(
                 out=x_codes[:, lo:hi].bitcast(FP8X4),
                 scales=x_scales[:, lo:hi],
@@ -105,163 +144,206 @@ def tile_moe_tk_glu_silu_kernel(
 
         interleave(nc.scalar.copy, 0, 128)
         interleave(nc.vector.tensor_copy, 128, 256)
-        quantise(128, 256)
-        quantise(0, 128)
-        interleave(nc.scalar.copy, 448, 512)
+        quantise_tokens(128, 256)
+        quantise_tokens(0, 128)
+        interleave(nc.scalar.copy, 416, 512)
         interleave(nc.vector.tensor_copy, 256, 384)
-        interleave(nc.vector.tensor_copy, 384, 448)
-        quantise(256, 384)
-        quantise(384, 512)
+        interleave(nc.vector.tensor_copy, 384, 416)
+        quantise_tokens(256, 384)
+        quantise_tokens(384, 512)
 
         gathered = {}
-        runs = [[0,256],[256,512],[512,1024],[1024,1536],[1536,2048]]
-        first = {}
-        hidden = {}
-        turned = {}
-        second = {}
-        gated = {}
-        pooled = 5
-
-        def gather(g):
-            lo, hi = runs[g]
-            codes = keep.tile([P, hi - lo], U32, name=f"codes{g}", align_bytes=64)
-            scales = keep.tile([P, hi - lo], U8, name=f"scales{g}", align_bytes=64)
+        for lo, hi in RUNS:
+            codes = keep.tile([P, hi - lo], U32, name=f"codes{lo}", align_bytes=64)
+            scales = keep.tile([P, hi - lo], U8, name=f"scales{lo}", align_bytes=64)
             mine = offsets[:, lo // 16 : hi // 16]
             nc.vector.tensor_copy(codes[:], x_codes[:].indirect(mine))
             nc.vector.tensor_copy(scales[:], x_scales[:].indirect(mine))
-            for t in range(lo // P, hi // P):
-                cols = slice(t * P - lo, t * P - lo + P)
-                gathered[t] = (codes[:, cols], scales[:, cols])
+            for batch in range(lo // P, hi // P):
+                cols = slice(batch * P - lo, batch * P - lo + P)
+                gathered[batch] = (codes[:, cols], scales[:, cols])
 
-        def product(bank, t, words, plane):
-            e = t // 2
-            codes, scales = gathered[t]
-            if e == 5 and words is words1:
-                moving = words1_5[:, 0, :]
+        pair_a = [keep.tile([P, 2, H], F32, name=f"pair_a{e}") for e in range(POOLED)]
+        pair_b = [keep.tile([P, 2, H], F32, name=f"pair_b{e}", align_bytes=64) for e in range(POOLED)]
+        h_rows = keep.tile([P, E * C * 4], BF16, name="h_rows", align_bytes=64)
+        h_own = keep.tile([P, 2, H], BF16, name="h_own", align_bytes=64)
+        arrived = {"a": (pairs1, plane1), "b": (pairs3, plane3)}
+        placed = {"a": moved_plane1, "b": moved_plane3}
+        number = {}
+        waiting = {}
+        activated = {}
+        hidden = {}
+        turned = {}
+
+        def product(matrix, batch, bank_number):
+            number[matrix, batch] = bank_number
+            bank = psum.tile([P, H], F32, name=f"bank{bank_number}")
+            e = batch // 2
+            codes, scales = gathered[batch]
+            if e < TURNED:
+                pairs, plane = arrived[matrix]
+                nc.tensor.matmul_mx(
+                    out=bank[:],
+                    lhsT=codes.bitcast(FP8X4),
+                    lhsT_scale=scales,
+                    rhs=pairs[e - e % 2][:, e % 2, :].bitcast(FP4X4),
+                    rhs_scale=plane[:, e, :],
+                    start=True,
+                    stop=True,
+                )
             else:
-                moving = words[e // 2][:, e % 2, :]
-            nc.tensor.matmul_mx(
-                out=bank[:],
-                lhsT=codes.bitcast(FP8X4),
-                lhsT_scale=scales,
-                rhs=moving.bitcast(FP4X4),
-                rhs_scale=plane[:, e, :],
-                start=True,
-                stop=True,
+                for j in range(4):
+                    nc.tensor.matmul_mx(
+                        out=bank[:, j * P : (j + 1) * P],
+                        lhsT=moved[matrix, e][:, 2 * j * P : 2 * (j + 1) * P].bitcast(FP4X4),
+                        lhsT_scale=placed[matrix][:, e - TURNED, j * P : (j + 1) * P],
+                        rhs=codes.bitcast(FP8X4),
+                        rhs_scale=scales,
+                        start=True,
+                        stop=True,
+                    )
+            return bank
+
+        def in_bank(batch, bank):
+            if batch < 2 * TURNED:
+                return bank[:].rearrange("p (m u d) -> p u m d", u=2, d=2)
+            return bank[:].rearrange("p (j s) -> p s j", j=4)
+
+        def in_row(batch, row):
+            if batch < 2 * TURNED:
+                return row.rearrange("p (u m d) -> p u m d", u=2, d=2)
+            return row.rearrange("p (s j) -> p s j", j=4)
+
+        def activate(batch, bank_number):
+            a = product("a", batch, bank_number)
+            if batch < 2 * POOLED:
+                row = pair_a[batch // 2][:, batch % 2, :]
+            else:
+                own = keep.tile([P, H], F32, name=f"silu{batch}", align_bytes=64)
+                row = own[:]
+            nc.scalar.activation(in_row(batch, row), in_bank(batch, a), SILU)
+            activated[batch] = row
+
+        def linear(batch, bank_number):
+            waiting[batch] = product("b", batch, bank_number)
+
+        def unload(batch):
+            nc.scalar.copy(in_row(batch, pair_b[batch // 2][:, batch % 2, :]), in_bank(batch, waiting.pop(batch)))
+
+        def multiply(batch):
+            if batch < 2 * TURNED:
+                h = h_own[:, batch % 2, :]
+                hidden[batch] = h
+            else:
+                start = (2 * PLACES.index(batch // 2) + batch % 2) * H
+                h = h_rows[:, start : start + H]
+            nc.vector.tensor_tensor(
+                in_row(batch, h), in_bank(batch, waiting.pop(batch)), in_row(batch, activated.pop(batch)), MULT
             )
 
-        def split(t):
-            return t[:].rearrange("p (m u d) -> p u m d", u=2, d=2)
+        def multiply_pooled(e, h):
+            nc.gpsimd.tensor_tensor(h, pair_b[e][:], pair_a[e][:], MULT)
+            hidden[2 * e] = h[:, 0, :]
+            hidden[2 * e + 1] = h[:, 1, :]
 
-        def pieces(t):
-            return t[:].rearrange("p (u m d) -> p u m d", u=2, d=2)
-
-        def activate(t, bank):
-            a = psum.tile([P, H], F32, name=f"bank{bank}")
-            product(a, t, words1, plane1)
-            if t == 2 * E - 1:
-                sa = keep.tile([P, H], F32, name="after_last_product", align_bytes=64)
-            else:
-                sa = wide.tile([P, H], F32, name="sa")
-            nc.scalar.activation(pieces(sa), split(a), SILU)
-            gated[t] = sa
-
-        def linear(t, bank):
-            b = psum.tile([P, H], F32, name=f"bank{bank}")
-            product(b, t, words3, plane3)
-            if t < pooled:
-                if t == pooled - 1:
-                    sb = keep.tile([P, H], F32, name="after_gpsimd", align_bytes=64)
-                else:
-                    sb = wide.tile([P, H], F32, name="sb")
-                nc.scalar.copy(pieces(sb), split(b))
-                b = sb
-            first[t] = b
-
-        def glu(t):
-            h = h_all[:, t - pooled, :]
-            nc.vector.tensor_tensor(pieces(h), split(first.pop(t)), pieces(gated.pop(t)), MULT)
-            hidden[t] = h
-
-        def turn(e, number, copy):
-            bank = psum.tile([P, 2, 2, P], F32, name=f"bank{number}")
+        def turn(e, bank_number):
+            bank = psum.tile([P, 2, 2, P], F32, name=f"bank{bank_number}")
             for s in range(2):
                 h = hidden.pop(2 * e + s)
                 for u in range(2):
-                    nc.tensor.transpose(bank[:, s, u, :], h[:, u * 256 : (u + 1) * 256].bitcast(F32), ident[:])
-            rows = wide.tile([P, C * 4], BF16, name="rows", align_bytes=64)
-            copy(
-                rows[:].bitcast(F32).rearrange("p (s c u) -> p s c u", s=2, u=2), bank[:].rearrange("p s u c -> p s c u")
+                    nc.tensor.transpose(bank[:, s, u, :], h[:, u * H // 2 : (u + 1) * H // 2].bitcast(F32), ident[:])
+            turned[e] = bank
+
+        def empty(e):
+            rows = h_rows[:, PLACES.index(e) * C * 4 : (PLACES.index(e) + 1) * C * 4]
+            nc.scalar.copy(
+                rows.bitcast(F32).rearrange("p (s c u) -> p s c u", s=2, u=2),
+                turned.pop(e)[:].rearrange("p s u c -> p s c u"),
             )
-            turned[e] = rows
 
-        def layer2(e, bank):
-            mine = slice(e * C, (e + 1) * C)
-            nc.vector.quantize_mx(out=h_codes[:, mine].bitcast(FP8X4), scales=h_scales[:, mine], in_=turned.pop(e)[:])
-            y = psum.tile([P, C], F32, name=f"bank{bank}")
-            nc.tensor.matmul_mx(
-                out=y[:],
-                lhsT=words2[:, e, :].bitcast(FP4X4),
-                lhsT_scale=plane2[:, e, :],
-                rhs=h_codes[:, mine].bitcast(FP8X4),
-                rhs_scale=h_scales[:, mine],
-                start=True,
-                stop=True,
+        activate(0, 2)
+        activate(1, 3)
+        for batch, bank_number in ((0, 6), (1, 7), (2, 4), (3, 5)):
+            linear(batch, bank_number)
+            unload(batch)
+        activate(2, number["b", 0])
+        activate(3, number["b", 1])
+        h_first = keep.tile([P, 2, H], BF16, name="h_first", align_bytes=64)
+        multiply_pooled(0, h_first[:])
+        permute(late_words, (("a", 6), ("a", 7), ("b", 6), ("b", 7)))
+        h_later = keep.tile([P, 4, H], BF16, name="late_words", align_bytes=64)
+        multiply_pooled(1, h_later[:, 0:2, :])
+        for batch in range(4, 8):
+            activate(batch, batch - 4)
+        for batch in range(4, 8):
+            linear(batch, batch)
+        unload(4)
+        unload(5)
+        multiply_pooled(2, h_later[:, 2:4, :])
+        activate(8, number["a", 4])
+        activate(9, number["a", 5])
+        linear(8, number["a", 6])
+        linear(9, number["a", 7])
+        activate(10, number["b", 4])
+        multiply(6)
+        activate(11, number["b", 6])
+        linear(10, number["b", 5])
+        multiply(7)
+        activate(12, number["b", 7])
+        linear(11, number["a", 8])
+        activate(13, number["a", 9])
+        multiply(8)
+        linear(12, number["b", 8])
+        activate(14, number["a", 10])
+        multiply(9)
+        linear(13, number["b", 9])
+        activate(15, number["a", 11])
+        multiply(10)
+        linear(14, number["b", 10])
+        linear(15, number["a", 12])
+        multiply(11)
+        turn_order = [e for e in PLACES if e < TURNED]
+        for batch, e in zip(range(12, 16), turn_order):
+            multiply(batch)
+            turn(e, number["b", batch])
+        for e in turn_order:
+            empty(e)
+
+        y_all = keep.tile([P, S], F32, name="late_words", align_bytes=64)
+        h_codes = keep.tile([P, S], U32, name=f"pair_b{POOLED - 1}", align_bytes=64)
+        h_scales = keep.tile([P, S], U8, name="silu14", align_bytes=64)
+        groups = (
+            (0, 2, number["b", 11], nc.scalar.copy),
+            (2, 4, number["a", 13], nc.scalar.copy),
+            (4, 6, number["a", 14], nc.scalar.copy),
+            (6, 7, number["a", 15], nc.vector.tensor_copy),
+            (7, 8, number["b", 12], nc.scalar.copy),
+        )
+        for lo, hi, bank_number, copy in groups:
+            nc.vector.quantize_mx(
+                out=h_codes[:, lo * C : hi * C].bitcast(FP8X4),
+                scales=h_scales[:, lo * C : hi * C],
+                in_=h_rows[:, lo * C * 4 : hi * C * 4],
             )
-            second[e] = y
-
-        def collect(e, copy):
-            copy(y_all[:, e * C : (e + 1) * C], second.pop(e)[:])
-
-        tiles = 2 * E
-        scalar_copy = nc.scalar.copy
-        vector_copy = nc.vector.tensor_copy
-        for g in range(len(runs)):
-            gather(g)
-        for pair in range(2):
-            for i in range(2):
-                activate(2 * pair + i, 4 * pair + i)
-            for i in range(2):
-                linear(2 * pair + i, 4 * pair + 2 + i)
-        activate(4, 0)
-        linear(4, 1)
-        for t in range(5, 8):
-            activate(t, t - 3)
-        for t in range(5, 8):
-            linear(t, t)
-        activate(8, 0)
-        linear(8, 1)
-        for t in range(9, 12):
-            activate(t, t - 7)
-        h_all = keep.tile([P, tiles - pooled, H], BF16, name="after_w1_of_tile_9", align_bytes=64)
-        a_banks = {12: 5, 13: 6, 14: 7, 15: 1}
-        b_banks = {9: 0, 10: 2, 11: 3, 12: 4, 13: 0, 14: 2, 15: 3}
-        for t in range(pooled, tiles):
-            if t in b_banks:
-                linear(t, b_banks[t])
-            glu(t)
-            if t + 7 < tiles:
-                activate(t + 7, a_banks[t + 7])
-            if t == pooled:
-                h_pooled = keep.tile([P, pooled, H], BF16, name="h_pooled", align_bytes=64)
-                for i in range(pooled):
-                    nc.gpsimd.tensor_tensor(h_pooled[:, i, :], first.pop(i)[:], gated.pop(i)[:], MULT)
-                    hidden[i] = h_pooled[:, i, :]
-        h_codes = keep.tile([P, S], U32, name="after_gpsimd", align_bytes=64)
-        h_scales = keep.tile([P, S], U8, name="after_last_product", align_bytes=64)
-        for e, bank in ((3, 5), (0, 6)):
-            turn(e, bank, scalar_copy)
-        turn(5, 4, vector_copy)
-        for e, bank in ((4, 7), (1, 1)):
-            turn(e, bank, scalar_copy)
-        for e, bank in ((6, 0), (2, 2), (7, 3)):
-            turn(e, bank, scalar_copy)
-        for e, bank in ((3, 5), (0, 6), (4, 7), (5, 4), (1, 1), (6, 0), (2, 2), (7, 3)):
-            layer2(e, bank)
-        for e in (3, 0, 4, 5, 1):
-            collect(e, scalar_copy)
-        for e in (6, 2, 7):
-            collect(e, vector_copy)
+        results = []
+        for lo, hi, bank_number, copy in groups:
+            y = psum.tile([P, hi - lo, C], F32, name=f"bank{bank_number}")
+            for n in range(lo, hi):
+                mine = slice(n * C, (n + 1) * C)
+                nc.tensor.matmul_mx(
+                    out=y[:, n - lo, :],
+                    lhsT=words2[:, PLACES[n], :].bitcast(FP4X4),
+                    lhsT_scale=plane2[:, PLACES[n], :],
+                    rhs=h_codes[:, mine].bitcast(FP8X4),
+                    rhs_scale=h_scales[:, mine],
+                    start=True,
+                    stop=True,
+                )
+            results.append(y)
+        by_expert = y_all[:].rearrange("p (e c) -> p e c", c=C)
+        for (lo, hi, bank_number, copy), y in zip(groups, results):
+            low, high = PLACES[lo], PLACES[hi - 1]
+            copy(by_expert[:, low : high + 1 : max(high - low, 1), :], y[:])
 
         parts = [keep.tile([P, T], F32, name=f"part{r}") for r in range(TOP)]
         turned_sum = keep.tile([P, T], F32, name="turned_sum")
@@ -284,24 +366,22 @@ def tile_moe_tk_glu_silu_kernel(
                     is_transpose=True,
                 )
 
-        def turn_back(cols):
-            bank = psum.tile([P, T // 2], F32, name=f"bank{4 + cols.start // (T // 2)}")
+        def turn_back(cols, bank):
             for b in range(cols.start // P, cols.stop // P):
                 block = slice(b * P, (b + 1) * P)
                 nc.scalar.copy(turned_sum[:, block], sums[b][:])
-                nc.tensor.transpose(bank[:, b * P - cols.start : (b + 1) * P - cols.start], turned_sum[:, block], ident[:])
-            return bank
+                nc.tensor.transpose(bank[:, b % 2 * P : (b % 2 + 1) * P], turned_sum[:, block], ident[:])
 
         for r in range(TOP - 2):
             fetch(r, slice(0, T))
             add_turned(r, slice(0, T))
-        banks = []
-        for cols in halves:
+        back = [psum.tile([P, T // 2], F32, name=f"bank{T // P + i}") for i in range(2)]
+        for cols, bank in zip(halves, back):
             fetch(TOP - 2, cols)
             add_turned(TOP - 2, cols)
-            banks.append(turn_back(cols))
+            turn_back(cols, bank)
         for cols in halves:
             fetch(TOP - 1, cols)
-        for cols, bank in zip(halves, banks):
+        for cols, bank in zip(halves, back):
             nc.vector.tensor_tensor(total[:, cols], bank[:], parts[TOP - 1][:, cols], ADD)
             nc.sync.dma_start(out[:, cols], total[:, cols])

@@ -24,6 +24,7 @@ U8 = mybir.dt.uint8
 FP8X4 = mybir.dt.float8_e4m3fn_x4
 FP4X4 = mybir.dt.float4_e2m1fn_x4
 SILU = mybir.ActivationFunctionType.Silu
+COPY = mybir.ActivationFunctionType.Copy
 ADD = mybir.AluOpType.add
 MULT = mybir.AluOpType.mult
 
@@ -124,13 +125,18 @@ def tile_moe_tk_glu_silu_kernel(
             place(moved_plane1, first1, quadrant)
         permute(pairs3[4], (("b", 4), ("b", 5)))
         plane2 = keep.tile([P, E, N], U8, name="spread", align_bytes=64)
-        gates = keep.tile([P, TOP, T], F32, name="spread_moved", align_bytes=64)
+        gates = keep.tile([P, 2, T], F32, name="spread_moved", align_bytes=64)
         nc.gpsimd.memset(as_words(plane2), 0)
         load_plane(plane2, w2_scales, E)
         load_words(words2[:], w2_words, 0, E)
         for tile, pos in zip(positions, (pos1, pos2, pos3, pos4)):
             nc.sync.dma_start(tile[:], pos)
-        nc.sync.dma_start(gates[:], gate.rearrange("r p t -> p r t"))
+        nc.sync.dma_start(gates[:], gate.rearrange("r p t -> p r t")[:, 2:, :])
+        columns = [keep.tile([P, 2, 8], F32, name=f"columns{h}") for h in range(2)]
+        with nc.allow_non_contiguous_dma(reason="one gate a partition"):
+            for h in range(2):
+                for r in range(2):
+                    nc.sync.dma_start(columns[h][:, r, 0:2], gate[r, 0, :].rearrange("(h b p) -> h p b", h=2, b=2)[h])
 
         def interleave(copy, lo, hi):
             copy(x_rows[:, lo:hi, :], x_raw[:, :, lo:hi].rearrange("p j t -> p t j"))
@@ -345,43 +351,62 @@ def tile_moe_tk_glu_silu_kernel(
             low, high = PLACES[lo], PLACES[hi - 1]
             copy(by_expert[:, low : high + 1 : max(high - low, 1), :], y[:])
 
-        parts = [keep.tile([P, T], F32, name=f"part{r}") for r in range(TOP)]
-        turned_sum = keep.tile([P, T], F32, name="turned_sum")
+        half = T // 2
+        halves = (slice(0, half), slice(half, T))
         total = keep.tile([P, T], F32, name="total")
-        halves = (slice(0, T // 2), slice(T // 2, T))
-        sums = [psum.tile([P, P], F32, name=f"bank{b}") for b in range(T // P)]
+        third = keep.tile([P, T], F32, name="third")
+        both = keep.tile([P, T], F32, name="both")
+        gated = [keep.tile([P, 2, 2, P], F32, name=f"gated{h}") for h in range(2)]
+        back = [psum.tile([P, half], F32, name=f"bank{h}") for h in range(2)]
 
-        def fetch(r, cols):
-            mine = positions[r][:, cols.start // 16 : cols.stop // 16]
-            nc.vector.tensor_tensor(parts[r][:, cols], y_all[:].indirect(mine), gates[:, r, cols], MULT)
+        def slots_of(r, cols):
+            return y_all[:].indirect(positions[r][:, cols.start // 16 : cols.stop // 16])
 
-        def add_turned(r, cols):
-            for b in range(cols.start // P, cols.stop // P):
-                nc.tensor.matmul(
-                    sums[b][:],
-                    parts[r][:, b * P : (b + 1) * P],
-                    ident[:],
-                    start=(r == 0),
-                    stop=(r == TOP - 2),
-                    is_transpose=True,
-                )
+        def pick(r, h, bank):
+            picked = keep.tile([P, half], F32, name=f"picked{r}_{h}")
+            nc.scalar.activation(picked[:], slots_of(r, halves[h]), COPY)
+            for b in range(2):
+                nc.tensor.transpose(bank[:, b, :], picked[:, b * P : (b + 1) * P], ident[:])
 
-        def turn_back(cols, bank):
-            for b in range(cols.start // P, cols.stop // P):
-                block = slice(b * P, (b + 1) * P)
-                nc.scalar.copy(turned_sum[:, block], sums[b][:])
-                nc.tensor.transpose(bank[:, b % 2 * P : (b % 2 + 1) * P], turned_sum[:, block], ident[:])
+        def turn_back(h):
+            for b in range(2):
+                for r in range(2):
+                    nc.tensor.matmul(
+                        back[h][:, b * P : (b + 1) * P],
+                        gated[h][:, r, b, :],
+                        ident[:],
+                        start=(r == 0),
+                        stop=(r == 1),
+                        is_transpose=True,
+                    )
 
-        for r in range(TOP - 2):
-            fetch(r, slice(0, T))
-            add_turned(r, slice(0, T))
-        back = [psum.tile([P, T // 2], F32, name=f"bank{T // P + i}") for i in range(2)]
-        for cols, bank in zip(halves, back):
-            fetch(TOP - 2, cols)
-            add_turned(TOP - 2, cols)
-            turn_back(cols, bank)
-        for cols in halves:
-            fetch(TOP - 1, cols)
-        for cols, bank in zip(halves, back):
-            nc.vector.tensor_tensor(total[:, cols], bank[:], parts[TOP - 1][:, cols], ADD)
+        def fetch(part, r, cols):
+            nc.vector.tensor_tensor(part, slots_of(r, cols), gates[:, r - 2, cols], MULT)
+
+        early = psum.tile([P, 2, 2, P], F32, name="bank2")
+        late = [psum.tile([P, 2, P], F32, name=f"bank{3 + r}") for r in range(2)]
+        for r in range(2):
+            pick(r, 0, early[:, r])
+        for r in range(2):
+            pick(r, 1, late[r])
+        fetch(third[:], 2, slice(0, T))
+        fourth = [keep.tile([P, half], F32, name="fourth")]
+        fetch(fourth[0][:], 3, halves[0])
+        nc.vector.tensor_tensor(
+            gated[0][:],
+            early[:],
+            columns[0][:, :, 0:2].unsqueeze(3).to_broadcast([P, 2, 2, P]),
+            MULT,
+        )
+        turn_back(0)
+        fourth.append(keep.tile([P, half], F32, name="columns0"))
+        fetch(fourth[1][:], 3, halves[1])
+        for r in range(2):
+            for b in range(2):
+                nc.scalar.activation(gated[1][:, r, b, :], late[r][:, b, :], COPY, scale=columns[1][:, r, b : b + 1])
+        turn_back(1)
+        for h, cols in enumerate(halves):
+            nc.vector.tensor_tensor(both[:, cols], third[:, cols], fourth[h][:], ADD)
+        for h, cols in enumerate(halves):
+            nc.vector.tensor_tensor(total[:, cols], back[h][:], both[:, cols], ADD)
             nc.sync.dma_start(out[:, cols], total[:, cols])

@@ -125,18 +125,21 @@ def tile_moe_tk_glu_silu_kernel(
             place(moved_plane1, first1, quadrant)
         permute(pairs3[4], (("b", 4), ("b", 5)))
         plane2 = keep.tile([P, E, N], U8, name="spread", align_bytes=64)
-        gates = keep.tile([P, 2, T], F32, name="spread_moved", align_bytes=64)
+        gates = keep.tile([P, 2 * T + 2 * P], F32, name="spread_moved", align_bytes=64)
         nc.gpsimd.memset(as_words(plane2), 0)
         load_plane(plane2, w2_scales, E)
         load_words(words2[:], w2_words, 0, E)
         for tile, pos in zip(positions, (pos1, pos2, pos3, pos4)):
             nc.sync.dma_start(tile[:], pos)
-        nc.sync.dma_start(gates[:], gate.rearrange("r p t -> p r t")[:, 2:, :])
-        columns = [keep.tile([P, 2, 8], F32, name=f"columns{h}") for h in range(2)]
+        by_choice = gate.rearrange("r p t -> p r t")
+        gates_fused = gates[:, : 2 * T].rearrange("p (r t) -> p r t", r=2)
+        gates_first = gates[:, 2 * T :].rearrange("p (r t) -> p r t", r=2)
+        nc.sync.dma_start(gates_fused, by_choice[:, 2:, :])
+        nc.sync.dma_start(gates_first, by_choice[:, 0:2, :P])
+        columns = keep.tile([P, 2, 8], F32, name="columns")
         with nc.allow_non_contiguous_dma(reason="one gate a partition"):
-            for h in range(2):
-                for r in range(2):
-                    nc.sync.dma_start(columns[h][:, r, 0:2], gate[r, 0, :].rearrange("(h b p) -> h p b", h=2, b=2)[h])
+            for r in range(2):
+                nc.sync.dma_start(columns[:, r, 0:3], gate[r, 0, P:].rearrange("(b p) -> p b", b=3))
 
         def interleave(copy, lo, hi):
             copy(x_rows[:, lo:hi, :], x_raw[:, :, lo:hi].rearrange("p j t -> p t j"))
@@ -351,62 +354,43 @@ def tile_moe_tk_glu_silu_kernel(
             low, high = PLACES[lo], PLACES[hi - 1]
             copy(by_expert[:, low : high + 1 : max(high - low, 1), :], y[:])
 
-        half = T // 2
-        halves = (slice(0, half), slice(half, T))
+        blocks = T // P - 1
+        first, rest = slice(0, P), slice(P, T)
         total = keep.tile([P, T], F32, name="total")
-        third = keep.tile([P, T], F32, name="third")
-        both = keep.tile([P, T], F32, name="both")
-        gated = [keep.tile([P, 2, 2, P], F32, name=f"gated{h}") for h in range(2)]
-        back = [psum.tile([P, half], F32, name=f"bank{h}") for h in range(2)]
+        fetched = keep.tile([P, 2, T], F32, name="fetched")
+        picked = keep.tile([P, 2, P], F32, name="picked")
+        weighed = keep.tile([P, 2, P], F32, name="weighed")
+        paired = keep.tile([P, 2, P], F32, name="paired")
+        both = keep.tile([P, blocks, P], F32, name="both")
+        gated = keep.tile([P, 2, blocks, P], F32, name="gated")
+        across = [psum.tile([P, blocks, P], F32, name=f"bank{r}") for r in range(2)]
+        back = [psum.tile([P, P], F32, name=f"bank{2 + b}") for b in range(blocks)]
 
         def slots_of(r, cols):
             return y_all[:].indirect(positions[r][:, cols.start // 16 : cols.stop // 16])
 
-        def pick(r, h, bank):
-            picked = keep.tile([P, half], F32, name=f"picked{r}_{h}")
-            nc.scalar.activation(picked[:], slots_of(r, halves[h]), COPY)
-            for b in range(2):
-                nc.tensor.transpose(bank[:, b, :], picked[:, b * P : (b + 1) * P], ident[:])
-
-        def turn_back(h):
-            for b in range(2):
-                for r in range(2):
-                    nc.tensor.matmul(
-                        back[h][:, b * P : (b + 1) * P],
-                        gated[h][:, r, b, :],
-                        ident[:],
-                        start=(r == 0),
-                        stop=(r == 1),
-                        is_transpose=True,
-                    )
-
-        def fetch(part, r, cols):
-            nc.vector.tensor_tensor(part, slots_of(r, cols), gates[:, r - 2, cols], MULT)
-
-        early = psum.tile([P, 2, 2, P], F32, name="bank2")
-        late = [psum.tile([P, 2, P], F32, name=f"bank{3 + r}") for r in range(2)]
         for r in range(2):
-            pick(r, 0, early[:, r])
+            plain = keep.tile([P, blocks * P], F32, name=f"plain{r}")
+            nc.scalar.activation(plain[:], slots_of(r, rest), COPY)
+            for b in range(blocks):
+                nc.tensor.transpose(across[r][:, b, :], plain[:, b * P : (b + 1) * P], ident[:])
         for r in range(2):
-            pick(r, 1, late[r])
-        fetch(third[:], 2, slice(0, T))
-        fourth = [keep.tile([P, half], F32, name="fourth")]
-        fetch(fourth[0][:], 3, halves[0])
-        nc.vector.tensor_tensor(
-            gated[0][:],
-            early[:],
-            columns[0][:, :, 0:2].unsqueeze(3).to_broadcast([P, 2, 2, P]),
-            MULT,
-        )
-        turn_back(0)
-        fourth.append(keep.tile([P, half], F32, name="columns0"))
-        fetch(fourth[1][:], 3, halves[1])
+            nc.scalar.activation(picked[:, r, :], slots_of(r, first), COPY)
+        for b in range(blocks):
+            for r in range(2):
+                nc.scalar.activation(gated[:, r, b, :], across[r][:, b, :], COPY, scale=columns[:, r, b : b + 1])
+                nc.tensor.matmul(
+                    back[b][:], gated[:, r, b, :], ident[:], start=(r == 0), stop=(r == 1), is_transpose=True
+                )
         for r in range(2):
-            for b in range(2):
-                nc.scalar.activation(gated[1][:, r, b, :], late[r][:, b, :], COPY, scale=columns[1][:, r, b : b + 1])
-        turn_back(1)
-        for h, cols in enumerate(halves):
-            nc.vector.tensor_tensor(both[:, cols], third[:, cols], fourth[h][:], ADD)
-        for h, cols in enumerate(halves):
-            nc.vector.tensor_tensor(total[:, cols], back[h][:], both[:, cols], ADD)
+            nc.vector.tensor_tensor(fetched[:, r, :], slots_of(2 + r, slice(0, T)), gates_fused[:, r, :], MULT)
+        nc.vector.tensor_tensor(weighed[:], picked[:], gates_first, MULT)
+        nc.vector.tensor_tensor(both[:].rearrange("p b t -> p (b t)"), fetched[:, 0, rest], fetched[:, 1, rest], ADD)
+        nc.vector.tensor_tensor(paired[:], weighed[:], fetched[:, :, first], ADD)
+        for b in range(blocks):
+            cols = slice((b + 1) * P, (b + 2) * P)
+            nc.vector.tensor_tensor(total[:, cols], back[b][:], both[:, b, :], ADD)
+            if b == 0:
+                nc.vector.tensor_tensor(total[:, first], paired[:, 0, :], paired[:, 1, :], ADD)
+                cols = slice(0, 2 * P)
             nc.sync.dma_start(out[:, cols], total[:, cols])

@@ -358,7 +358,6 @@ def tile_moe_tk_glu_silu_kernel(
         first, rest = slice(0, P), slice(P, T)
         total = keep.tile([P, T], F32, name="total")
         fetched = keep.tile([P, 2, T], F32, name="fetched")
-        picked = keep.tile([P, 2, P], F32, name="picked")
         weighed = keep.tile([P, 2, P], F32, name="weighed")
         paired = keep.tile([P, 2, P], F32, name="paired")
         both = keep.tile([P, blocks, P], F32, name="both")
@@ -374,8 +373,6 @@ def tile_moe_tk_glu_silu_kernel(
             nc.scalar.activation(plain[:], slots_of(r, rest), COPY)
             for b in range(blocks):
                 nc.tensor.transpose(across[r][:, b, :], plain[:, b * P : (b + 1) * P], ident[:])
-        for r in range(2):
-            nc.scalar.activation(picked[:, r, :], slots_of(r, first), COPY)
         for b in range(blocks):
             for r in range(2):
                 nc.scalar.activation(gated[:, r, b, :], across[r][:, b, :], COPY, scale=columns[:, r, b : b + 1])
@@ -384,7 +381,8 @@ def tile_moe_tk_glu_silu_kernel(
                 )
         for r in range(2):
             nc.vector.tensor_tensor(fetched[:, r, :], slots_of(2 + r, slice(0, T)), gates_fused[:, r, :], MULT)
-        nc.vector.tensor_tensor(weighed[:], picked[:], gates_first, MULT)
+        for r in range(2):
+            nc.vector.tensor_tensor(weighed[:, r, :], slots_of(r, first), gates_first[:, r, :], MULT)
         nc.vector.tensor_tensor(both[:].rearrange("p b t -> p (b t)"), fetched[:, 0, rest], fetched[:, 1, rest], ADD)
         nc.vector.tensor_tensor(paired[:], weighed[:], fetched[:, :, first], ADD)
         for b in range(blocks):

@@ -357,13 +357,13 @@ def tile_moe_tk_glu_silu_kernel(
         blocks = T // P - 1
         first, rest = slice(0, P), slice(P, T)
         total = keep.tile([P, T], F32, name="total")
-        fetched = keep.tile([P, 2, T], F32, name="fetched")
-        weighed = keep.tile([P, 2, P], F32, name="weighed")
-        paired = keep.tile([P, 2, P], F32, name="paired")
-        both = keep.tile([P, blocks, P], F32, name="both")
+        fetched = keep.tile([P, 2, T + P], F32, name="fetched")
+        both = keep.tile([P, T + P], F32, name="both")
         gated = keep.tile([P, 2, blocks, P], F32, name="gated")
-        across = [psum.tile([P, blocks, P], F32, name=f"bank{r}") for r in range(2)]
-        back = [psum.tile([P, P], F32, name=f"bank{2 + b}") for b in range(blocks)]
+        shared = psum.tile([P, blocks, P], F32, name="bank0")
+        single = [psum.tile([P, P], F32, name=f"bank{1 + b}") for b in range(blocks)]
+        across = ([shared[:, b, :] for b in range(blocks)], [bank[:] for bank in single])
+        back = [psum.tile([P, P], F32, name=f"bank{1 + blocks + b}") for b in range(blocks)]
 
         def slots_of(r, cols):
             return y_all[:].indirect(positions[r][:, cols.start // 16 : cols.stop // 16])
@@ -372,23 +372,23 @@ def tile_moe_tk_glu_silu_kernel(
             plain = keep.tile([P, blocks * P], F32, name=f"plain{r}")
             nc.scalar.activation(plain[:], slots_of(r, rest), COPY)
             for b in range(blocks):
-                nc.tensor.transpose(across[r][:, b, :], plain[:, b * P : (b + 1) * P], ident[:])
-        for b in range(blocks):
-            for r in range(2):
-                nc.scalar.activation(gated[:, r, b, :], across[r][:, b, :], COPY, scale=columns[:, r, b : b + 1])
+                nc.tensor.transpose(across[r][b], plain[:, b * P : (b + 1) * P], ident[:])
+        for r in range(2):
+            for b in range(blocks):
+                nc.scalar.activation(gated[:, r, b, :], across[r][b], COPY, scale=columns[:, r, b : b + 1])
                 nc.tensor.matmul(
                     back[b][:], gated[:, r, b, :], ident[:], start=(r == 0), stop=(r == 1), is_transpose=True
                 )
         for r in range(2):
-            nc.vector.tensor_tensor(fetched[:, r, :], slots_of(2 + r, slice(0, T)), gates_fused[:, r, :], MULT)
+            nc.vector.tensor_tensor(fetched[:, r, :T], slots_of(2 + r, slice(0, T)), gates_fused[:, r, :], MULT)
         for r in range(2):
-            nc.vector.tensor_tensor(weighed[:, r, :], slots_of(r, first), gates_first[:, r, :], MULT)
-        nc.vector.tensor_tensor(both[:].rearrange("p b t -> p (b t)"), fetched[:, 0, rest], fetched[:, 1, rest], ADD)
-        nc.vector.tensor_tensor(paired[:], weighed[:], fetched[:, :, first], ADD)
+            nc.vector.tensor_tensor(fetched[:, r, T:], slots_of(r, first), gates_first[:, r, :], MULT)
+        nc.vector.tensor_tensor(both[:, :T], fetched[:, 0, :T], fetched[:, 1, :T], ADD)
+        nc.vector.tensor_tensor(both[:, T:], fetched[:, 0, T:], fetched[:, 1, T:], ADD)
         for b in range(blocks):
             cols = slice((b + 1) * P, (b + 2) * P)
-            nc.vector.tensor_tensor(total[:, cols], back[b][:], both[:, b, :], ADD)
+            nc.vector.tensor_tensor(total[:, cols], back[b][:], both[:, cols], ADD)
             if b == 0:
-                nc.vector.tensor_tensor(total[:, first], paired[:, 0, :], paired[:, 1, :], ADD)
+                nc.vector.tensor_tensor(total[:, first], both[:, first], both[:, T:], ADD)
                 cols = slice(0, 2 * P)
             nc.sync.dma_start(out[:, cols], total[:, cols])

@@ -12,7 +12,7 @@ TURNED = 4
 DIRECT = E - TURNED
 POOLED = 3
 BLOCKS = K // 32
-RUNS = ((0, 256), (256, 512), (512, 1024), (1024, 1536), (1536, 2048))
+RUNS = ((0, 128), (128, 384), (384, 896), (896, 1408), (1408, 2048))
 PLACES = (4, 5, 0, 6, 3, 7, 1, 2)
 
 F32 = mybir.dt.float32
@@ -48,6 +48,7 @@ def tile_moe_tk_glu_silu_kernel(
 
         plane1 = keep.tile([P, TURNED, H], U8, name="plane1", align_bytes=64)
         plane3 = keep.tile([P, TURNED, H], U8, name="plane3", align_bytes=64)
+        plane2 = keep.tile([P, E, N], U8, name="plane2", align_bytes=64)
         spread = keep.tile([P, H], U8, name="spread", align_bytes=64)
         spread_moved = keep.tile([P, H], U8, name="spread_moved", align_bytes=64)
         moved_plane1 = keep.tile([P, DIRECT, H], U8, name="moved_plane1", align_bytes=64)
@@ -74,7 +75,7 @@ def tile_moe_tk_glu_silu_kernel(
         nc.sync.dma_start(offsets[:], offs)
         nc.vector.memset(one[:], 0.0)
         nc.scalar.activation(one[:], one[:], SILU)
-        for plane in (plane1, plane3, moved_plane1, moved_plane3):
+        for plane in (plane3, plane1, moved_plane1, moved_plane3, plane2):
             nc.vector.memset(as_words(plane), 0)
         nc.gpsimd.memset(x_scales[:], 0)
         nc.gpsimd.memset(x_codes[:, T:], 0)
@@ -104,13 +105,13 @@ def tile_moe_tk_glu_silu_kernel(
             for i, key in enumerate(keys):
                 moved[key] = fresh[:, i, :]
 
-        load_plane(plane1, w1_scales, TURNED)
+        load_plane(plane3, w3_scales, TURNED)
+        load_words(pairs3[0][:], w3_words, 0, 2)
         load_words(pairs1[0][:], w1_words, 0, 2)
+        load_plane(plane1, w1_scales, TURNED)
         load_words(pairs1[4][:], w1_words, 4, 6)
         load_spread(w1_scales, first1)
         load_spread(w3_scales, first3)
-        load_plane(plane3, w3_scales, TURNED)
-        load_words(pairs3[0][:], w3_words, 0, 2)
         load_words(pairs3[4][:], w3_words, 4, 6)
         load_words(pairs3[2][:], w3_words, 2, 4)
         load_words(pairs1[2][:], w1_words, 2, 4)
@@ -124,9 +125,7 @@ def tile_moe_tk_glu_silu_kernel(
             place(moved_plane3, first3, quadrant)
             place(moved_plane1, first1, quadrant)
         permute(pairs3[4], (("b", 4), ("b", 5)))
-        plane2 = keep.tile([P, E, N], U8, name="spread", align_bytes=64)
         gates = keep.tile([P, 2 * T + 2 * P], F32, name="spread_moved", align_bytes=64)
-        nc.gpsimd.memset(as_words(plane2), 0)
         load_plane(plane2, w2_scales, E)
         load_words(words2[:], w2_words, 0, E)
         for tile, pos in zip(positions, (pos1, pos2, pos3, pos4)):
@@ -270,51 +269,61 @@ def tile_moe_tk_glu_silu_kernel(
                 turned.pop(e)[:].rearrange("p s u c -> p s c u"),
             )
 
-        activate(0, 2)
-        activate(1, 3)
-        for batch, bank_number in ((0, 6), (1, 7), (2, 4), (3, 5)):
-            linear(batch, bank_number)
-            unload(batch)
-        activate(2, number["b", 0])
-        activate(3, number["b", 1])
         h_first = keep.tile([P, 2, H], BF16, name="h_first", align_bytes=64)
+        linear(0, 0)
+        unload(0)
+        activate(0, 1)
+        activate(1, 2)
+        activate(2, 3)
+        linear(1, number["a", 0])
+        unload(1)
+        linear(2, number["a", 1])
+        unload(2)
         multiply_pooled(0, h_first[:])
         permute(late_words, (("a", 6), ("a", 7), ("b", 6), ("b", 7)))
         h_later = keep.tile([P, 4, H], BF16, name="late_words", align_bytes=64)
+        activate(3, number["b", 1])
+        linear(3, number["a", 2])
+        unload(3)
         multiply_pooled(1, h_later[:, 0:2, :])
-        for batch in range(4, 8):
-            activate(batch, batch - 4)
-        for batch in range(4, 8):
-            linear(batch, batch)
+        activate(4, number["b", 0])
+        linear(4, 4)
         unload(4)
+        activate(5, 5)
+        linear(5, 6)
         unload(5)
         multiply_pooled(2, h_later[:, 2:4, :])
+        activate(6, 7)
+        linear(6, number["b", 2])
+        activate(7, number["a", 3])
+        linear(7, number["b", 3])
         activate(8, number["a", 4])
-        activate(9, number["a", 5])
-        linear(8, number["a", 6])
-        linear(9, number["a", 7])
-        activate(10, number["b", 4])
+        activate(9, number["b", 4])
+        linear(8, number["a", 5])
+        linear(9, number["b", 5])
+        activate(10, number["a", 6])
+        activate(11, number["a", 7])
         multiply(6)
-        activate(11, number["b", 6])
-        linear(10, number["b", 5])
+        linear(10, number["a", 8])
+        activate(12, number["b", 6])
         multiply(7)
-        activate(12, number["b", 7])
-        linear(11, number["a", 8])
-        activate(13, number["a", 9])
+        linear(11, number["a", 9])
+        activate(13, number["b", 7])
         multiply(8)
-        linear(12, number["b", 8])
         activate(14, number["a", 10])
+        linear(12, number["b", 8])
         multiply(9)
-        linear(13, number["b", 9])
         activate(15, number["a", 11])
+        linear(13, number["b", 9])
         multiply(10)
         linear(14, number["b", 10])
         linear(15, number["a", 12])
         multiply(11)
-        turn_order = [e for e in PLACES if e < TURNED]
-        for batch, e in zip(range(12, 16), turn_order):
+        for batch in range(12, 16):
             multiply(batch)
-            turn(e, number["b", batch])
+        turn_order = [e for e in PLACES if e < TURNED]
+        for e, result in zip(turn_order, (("a", 13), ("a", 14), ("a", 15), ("b", 12))):
+            turn(e, number[result])
         for e in turn_order:
             empty(e)
 
@@ -322,27 +331,27 @@ def tile_moe_tk_glu_silu_kernel(
         h_codes = keep.tile([P, S], U32, name=f"pair_b{POOLED - 1}", align_bytes=64)
         h_scales = keep.tile([P, S], U8, name="silu14", align_bytes=64)
         groups = (
-            (0, 2, number["b", 11], nc.scalar.copy),
-            (2, 4, number["a", 13], nc.scalar.copy),
-            (4, 6, number["a", 14], nc.scalar.copy),
-            (6, 7, number["a", 15], nc.vector.tensor_copy),
-            (7, 8, number["b", 12], nc.scalar.copy),
+            (0, 2 * C, number["b", 11], nc.scalar.copy),
+            (2 * C, 4 * C, number["b", 13], nc.scalar.copy),
+            (4 * C, 6 * C, number["b", 14], nc.scalar.copy),
+            (6 * C, 7 * C, number["b", 15], nc.vector.tensor_copy),
+            (7 * C, 7 * C + P, number["a", 13], nc.scalar.copy),
+            (7 * C + P, 8 * C, number["a", 14], nc.scalar.copy),
         )
         for lo, hi, bank_number, copy in groups:
             nc.vector.quantize_mx(
-                out=h_codes[:, lo * C : hi * C].bitcast(FP8X4),
-                scales=h_scales[:, lo * C : hi * C],
-                in_=h_rows[:, lo * C * 4 : hi * C * 4],
+                out=h_codes[:, lo:hi].bitcast(FP8X4), scales=h_scales[:, lo:hi], in_=h_rows[:, lo * 4 : hi * 4]
             )
         results = []
         for lo, hi, bank_number, copy in groups:
-            y = psum.tile([P, hi - lo, C], F32, name=f"bank{bank_number}")
-            for n in range(lo, hi):
-                mine = slice(n * C, (n + 1) * C)
+            width = min(C, hi - lo)
+            y = psum.tile([P, (hi - lo) // width, width], F32, name=f"bank{bank_number}")
+            for i, start in enumerate(range(lo, hi, width)):
+                mine = slice(start, start + width)
                 nc.tensor.matmul_mx(
-                    out=y[:, n - lo, :],
-                    lhsT=words2[:, PLACES[n], :].bitcast(FP4X4),
-                    lhsT_scale=plane2[:, PLACES[n], :],
+                    out=y[:, i, :],
+                    lhsT=words2[:, PLACES[start // C], :].bitcast(FP4X4),
+                    lhsT_scale=plane2[:, PLACES[start // C], :],
                     rhs=h_codes[:, mine].bitcast(FP8X4),
                     rhs_scale=h_scales[:, mine],
                     start=True,
@@ -351,8 +360,8 @@ def tile_moe_tk_glu_silu_kernel(
             results.append(y)
         by_expert = y_all[:].rearrange("p (e c) -> p e c", c=C)
         for (lo, hi, bank_number, copy), y in zip(groups, results):
-            low, high = PLACES[lo], PLACES[hi - 1]
-            copy(by_expert[:, low : high + 1 : max(high - low, 1), :], y[:])
+            low, high = PLACES[lo // C], PLACES[(hi - 1) // C]
+            copy(by_expert[:, low : high + 1 : max(high - low, 1), lo % C : (hi - 1) % C + 1], y[:])
 
         blocks = T // P - 1
         first, rest = slice(0, P), slice(P, T)

@@ -11,7 +11,6 @@ FLOPS = 2 * S * (2 * K * H + H * N)
 TURNED = 4
 DIRECT = E - TURNED
 POOLED = 3
-BLOCKS = K // 32
 RUNS = ((0, 128), (128, 384), (384, 896), (896, 1408), (1408, 2048))
 PLACES = (4, 5, 0, 6, 3, 7, 1, 2)
 
@@ -44,19 +43,15 @@ def tile_moe_tk_glu_silu_kernel(
         x_codes = keep.tile([P, 2 * T], U32, name="x_codes", align_bytes=64)
         x_scales = keep.tile([P, 2 * T], U8, name="x_scales", align_bytes=64)
         ident = keep.tile([P, P], F32, name="ident")
-        one = keep.tile([P, 1], F32, name="one")
 
         plane1 = keep.tile([P, TURNED, H], U8, name="plane1", align_bytes=64)
         plane3 = keep.tile([P, TURNED, H], U8, name="plane3", align_bytes=64)
-        plane2 = keep.tile([P, E, N], U8, name="plane2", align_bytes=64)
         spread = keep.tile([P, H], U8, name="spread", align_bytes=64)
         spread_moved = keep.tile([P, H], U8, name="spread_moved", align_bytes=64)
-        moved_plane1 = keep.tile([P, DIRECT, H], U8, name="moved_plane1", align_bytes=64)
-        moved_plane3 = keep.tile([P, DIRECT, H], U8, name="moved_plane3", align_bytes=64)
+        moved_plane = keep.tile([P, 2 * DIRECT, H], U8, name="moved_plane", align_bytes=64)
         pairs1 = {lo: keep.tile([P, 2, 2 * H], U8, name=f"words1_{lo}", align_bytes=64) for lo in (0, 2, 4)}
         pairs3 = {lo: keep.tile([P, 2, 2 * H], U8, name=f"words3_{lo}", align_bytes=64) for lo in (0, 2, 4)}
         late_words = keep.tile([P, 4, 2 * H], U8, name="late_words", align_bytes=64)
-        words2 = keep.tile([P, E, 2 * N], U8, name="words2", align_bytes=64)
 
         def as_words(plane):
             return plane[:].rearrange("p e i -> p (e i)").bitcast(I32)
@@ -73,25 +68,20 @@ def tile_moe_tk_glu_silu_kernel(
         for lo in (0, T // 2):
             nc.sync.dma_start(x_raw[:, :, lo : lo + T // 2], x_view[:, :, lo : lo + T // 2])
         nc.sync.dma_start(offsets[:], offs)
-        nc.vector.memset(one[:], 0.0)
-        nc.scalar.activation(one[:], one[:], SILU)
-        for plane in (plane3, plane1, moved_plane1, moved_plane3, plane2):
+        nc.vector.memset(x_scales[:].bitcast(I32), 0)
+        for plane in (plane1, plane3, moved_plane):
             nc.vector.memset(as_words(plane), 0)
-        nc.gpsimd.memset(x_scales[:], 0)
         nc.gpsimd.memset(x_codes[:, T:], 0)
         make_identity(nc, ident[:])
 
-        first1, first3 = 0, BLOCKS * DIRECT
-
         def load_spread(scales, first):
             rows = scales.bitcast(I32).rearrange("e s q i -> q (e s) i")[:, TURNED:, :]
-            nc.sync.dma_start(spread[first : first + BLOCKS * DIRECT, :].bitcast(I32), rows)
+            nc.sync.dma_start(spread[first:P:2, :].bitcast(I32), rows)
 
-        def place(plane, first, quadrant):
-            start = first + quadrant * 4 * DIRECT
+        def place(quadrant):
             nc.sync.dma_start(
-                plane[32 * quadrant : 32 * quadrant + 4, :, :].bitcast(I32),
-                spread_moved[start : start + 4 * DIRECT, :].bitcast(I32),
+                moved_plane[32 * quadrant : 32 * quadrant + 4, :, :].bitcast(I32),
+                spread_moved[32 * quadrant : 32 * quadrant + 32, :].bitcast(I32),
             )
 
         moved = {}
@@ -105,13 +95,13 @@ def tile_moe_tk_glu_silu_kernel(
             for i, key in enumerate(keys):
                 moved[key] = fresh[:, i, :]
 
-        load_plane(plane3, w3_scales, TURNED)
-        load_words(pairs3[0][:], w3_words, 0, 2)
-        load_words(pairs1[0][:], w1_words, 0, 2)
         load_plane(plane1, w1_scales, TURNED)
+        load_words(pairs1[0][:], w1_words, 0, 2)
+        load_words(pairs3[0][:], w3_words, 0, 2)
         load_words(pairs1[4][:], w1_words, 4, 6)
-        load_spread(w1_scales, first1)
-        load_spread(w3_scales, first3)
+        load_plane(plane3, w3_scales, TURNED)
+        load_spread(w1_scales, 0)
+        load_spread(w3_scales, 1)
         load_words(pairs3[4][:], w3_words, 4, 6)
         load_words(pairs3[2][:], w3_words, 2, 4)
         load_words(pairs1[2][:], w1_words, 2, 4)
@@ -122,9 +112,11 @@ def tile_moe_tk_glu_silu_kernel(
             spread_moved[:].rearrange("p (j m) -> p j m", j=4), spread[:].rearrange("p (m j) -> p j m", j=4)
         )
         for quadrant in range(4):
-            place(moved_plane3, first3, quadrant)
-            place(moved_plane1, first1, quadrant)
+            place(quadrant)
         permute(pairs3[4], (("b", 4), ("b", 5)))
+        plane2 = keep.tile([P, E, N], U8, name="spread", align_bytes=64)
+        words2 = keep.tile([P, E, 2 * N], U8, name="words3_4", align_bytes=64)
+        nc.gpsimd.memset(as_words(plane2), 0)
         gates = keep.tile([P, 2 * T + 2 * P], F32, name="spread_moved", align_bytes=64)
         load_plane(plane2, w2_scales, E)
         load_words(words2[:], w2_words, 0, E)
@@ -135,10 +127,6 @@ def tile_moe_tk_glu_silu_kernel(
         gates_first = gates[:, 2 * T :].rearrange("p (r t) -> p r t", r=2)
         nc.sync.dma_start(gates_fused, by_choice[:, 2:, :])
         nc.sync.dma_start(gates_first, by_choice[:, 0:2, :P])
-        columns = keep.tile([P, 2, 8], F32, name="columns")
-        with nc.allow_non_contiguous_dma(reason="one gate a partition"):
-            for r in range(2):
-                nc.sync.dma_start(columns[:, r, 0:3], gate[r, 0, P:].rearrange("(b p) -> p b", b=3))
 
         def interleave(copy, lo, hi):
             copy(x_rows[:, lo:hi, :], x_raw[:, :, lo:hi].rearrange("p j t -> p t j"))
@@ -176,7 +164,7 @@ def tile_moe_tk_glu_silu_kernel(
         h_rows = keep.tile([P, E * C * 4], BF16, name="h_rows", align_bytes=64)
         h_own = keep.tile([P, 2, H], BF16, name="h_own", align_bytes=64)
         arrived = {"a": (pairs1, plane1), "b": (pairs3, plane3)}
-        placed = {"a": moved_plane1, "b": moved_plane3}
+        placed = {"a": 0, "b": 1}
         number = {}
         waiting = {}
         activated = {}
@@ -204,7 +192,7 @@ def tile_moe_tk_glu_silu_kernel(
                     nc.tensor.matmul_mx(
                         out=bank[:, j * P : (j + 1) * P],
                         lhsT=moved[matrix, e][:, 2 * j * P : 2 * (j + 1) * P].bitcast(FP4X4),
-                        lhsT_scale=placed[matrix][:, e - TURNED, j * P : (j + 1) * P],
+                        lhsT_scale=moved_plane[:, 2 * (e - TURNED) + placed[matrix], j * P : (j + 1) * P],
                         rhs=codes.bitcast(FP8X4),
                         rhs_scale=scales,
                         start=True,
@@ -270,23 +258,24 @@ def tile_moe_tk_glu_silu_kernel(
             )
 
         h_first = keep.tile([P, 2, H], BF16, name="h_first", align_bytes=64)
-        linear(0, 0)
-        unload(0)
-        activate(0, 1)
-        activate(1, 2)
-        activate(2, 3)
-        linear(1, number["a", 0])
-        unload(1)
-        linear(2, number["a", 1])
-        unload(2)
+        activate(0, 0)
+        for batch in range(3):
+            linear(batch, batch + 1)
+            unload(batch)
+        activate(1, number["b", 0])
+        activate(2, number["b", 1])
         multiply_pooled(0, h_first[:])
+        columns = keep.tile([P, 2, 8], F32, name="pair_a0")
+        with nc.allow_non_contiguous_dma(reason="one gate a partition"):
+            for r in range(2):
+                nc.sync.dma_start(columns[:, r, 0:3], gate[r, 0, P:].rearrange("(b p) -> p b", b=3))
         permute(late_words, (("a", 6), ("a", 7), ("b", 6), ("b", 7)))
         h_later = keep.tile([P, 4, H], BF16, name="late_words", align_bytes=64)
-        activate(3, number["b", 1])
-        linear(3, number["a", 2])
+        activate(3, number["a", 1])
+        linear(3, number["b", 2])
         unload(3)
         multiply_pooled(1, h_later[:, 0:2, :])
-        activate(4, number["b", 0])
+        activate(4, number["a", 0])
         linear(4, 4)
         unload(4)
         activate(5, 5)
@@ -294,7 +283,7 @@ def tile_moe_tk_glu_silu_kernel(
         unload(5)
         multiply_pooled(2, h_later[:, 2:4, :])
         activate(6, 7)
-        linear(6, number["b", 2])
+        linear(6, number["a", 2])
         activate(7, number["a", 3])
         linear(7, number["b", 3])
         activate(8, number["a", 4])

@@ -322,8 +322,8 @@ def tile_moe_tk_glu_silu_kernel(
         groups = (
             (0, 2 * C, number["b", 11], nc.scalar.copy),
             (2 * C, 4 * C, number["b", 13], nc.scalar.copy),
-            (4 * C, 6 * C, number["b", 14], nc.scalar.copy),
-            (6 * C, 7 * C, number["b", 15], nc.vector.tensor_copy),
+            (4 * C, 6 * C, number["b", 14], nc.vector.tensor_copy),
+            (6 * C, 7 * C, number["b", 15], nc.scalar.copy),
             (7 * C, 7 * C + P, number["a", 13], nc.scalar.copy),
             (7 * C + P, 8 * C, number["a", 14], nc.scalar.copy),
         )

from contextlib import ExitStack

import concourse.mybir as mybir
from concourse.masks import make_identity

T, E, C, K, H, N, TOP = 512, 8, 256, 512, 512, 128, 4
P = 128
S = E * C
FLOPS = 2 * S * (2 * K * H + H * N)

TURNED = 4
DIRECT = E - TURNED
POOLED = 3
RUNS = ((0, 128), (128, 384), (384, 896), (896, 1408), (1408, 2048))
PLACES = (4, 5, 0, 6, 3, 7, 1, 2)

F32 = mybir.dt.float32
BF16 = mybir.dt.bfloat16
I32 = mybir.dt.int32
U32 = mybir.dt.uint32
U16 = mybir.dt.uint16
U8 = mybir.dt.uint8
FP8X4 = mybir.dt.float8_e4m3fn_x4
FP4X4 = mybir.dt.float4_e2m1fn_x4
SILU = mybir.ActivationFunctionType.Silu
COPY = mybir.ActivationFunctionType.Copy
ADD = mybir.AluOpType.add
MULT = mybir.AluOpType.mult


def tile_moe_tk_glu_silu_kernel(
    tc, xT, w1_words, w1_scales, w3_words, w3_scales, w2_words, w2_scales, gate, offs, pos1, pos2, pos3, pos4, out
):
    nc = tc.nc
    with ExitStack() as ctx:
        keep = ctx.enter_context(tc.tile_pool(name="keep", bufs=1))
        psum = ctx.enter_context(tc.psum_pool(name="psum", bufs=1))

        offsets = keep.tile([P, S // 16], U16, name="offsets")
        positions = [keep.tile([P, T // 16], U16, name=f"positions{r}") for r in range(TOP)]
        x_raw = keep.tile([P, 4, T], F32, name="x_raw")
        x_rows = keep.tile([P, T, 4], BF16, name="x_rows", align_bytes=64)
        x_codes = keep.tile([P, 2 * T], U32, name="x_codes", align_bytes=64)
        x_scales = keep.tile([P, 2 * T], U8, name="x_scales", align_bytes=64)
        ident = keep.tile([P, P], F32, name="ident")

        plane1 = keep.tile([P, TURNED, H], U8, name="plane1", align_bytes=64)
        plane3 = keep.tile([P, TURNED, H], U8, name="plane3", align_bytes=64)
        spread = keep.tile([P, H], U8, name="spread", align_bytes=64)
        spread_moved = keep.tile([P, H], U8, name="spread_moved", align_bytes=64)
        moved_plane = keep.tile([P, 2 * DIRECT, H], U8, name="moved_plane", align_bytes=64)
        pairs1 = {lo: keep.tile([P, 2, 2 * H], U8, name=f"words1_{lo}", align_bytes=64) for lo in (0, 2, 4)}
        pairs3 = {lo: keep.tile([P, 2, 2 * H], U8, name=f"words3_{lo}", align_bytes=64) for lo in (0, 2, 4)}
        late_words = keep.tile([P, 4, 2 * H], U8, name="late_words", align_bytes=64)

        def as_words(plane):
            return plane[:].rearrange("p e i -> p (e i)").bitcast(I32)

        def load_plane(plane, scales, experts):
            rows = scales.bitcast(I32).rearrange("e s (q r) i -> r q (e s) i", r=4)
            for r in range(4):
                nc.sync.dma_start(plane[r:P:32, :, :].bitcast(I32), rows[r][:, :experts, :])

        def load_words(tile, words, lo, hi):
            nc.sync.dma_start(tile.bitcast(I32), words.bitcast(I32).rearrange("e s p i -> p (e s) i")[:, lo:hi, :])

        x_view = xT.rearrange("(p j) t -> p j t", j=4)
        for lo in (0, T // 2):
            nc.sync.dma_start(x_raw[:, :, lo : lo + T // 2], x_view[:, :, lo : lo + T // 2])
        nc.sync.dma_start(offsets[:], offs)
        nc.vector.memset(x_scales[:].bitcast(I32), 0)
        for plane in (plane1, plane3, moved_plane):
            nc.vector.memset(as_words(plane), 0)
        nc.gpsimd.memset(x_codes[:, T:], 0)
        make_identity(nc, ident[:])

        def load_spread(scales, first):
            rows = scales.bitcast(I32).rearrange("e s q i -> q (e s) i")[:, TURNED:, :]
            nc.sync.dma_start(spread[first:P:2, :].bitcast(I32), rows)

        def place(quadrant):
            nc.sync.dma_start(
                moved_plane[32 * quadrant : 32 * quadrant + 4, :, :].bitcast(I32),
                spread_moved[32 * quadrant : 32 * quadrant + 32, :].bitcast(I32),
            )

        moved = {}

        def permute(source, keys):
            fresh = keep.tile([P, len(keys), 2 * H], U8, name="moved_%s%d" % keys[0], align_bytes=64)
            nc.gpsimd.tensor_copy(
                fresh[:].bitcast(U16).rearrange("p e (j m) -> p e j m", j=4),
                source[:].bitcast(U16).rearrange("p e (m j) -> p e j m", j=4),
            )
            for i, key in enumerate(keys):
                moved[key] = fresh[:, i, :]

        load_plane(plane1, w1_scales, TURNED)
        load_words(pairs1[0][:], w1_words, 0, 2)
        load_words(pairs3[0][:], w3_words, 0, 2)
        load_words(pairs1[4][:], w1_words, 4, 6)
        load_plane(plane3, w3_scales, TURNED)
        load_spread(w1_scales, 0)
        load_spread(w3_scales, 1)
        load_words(pairs3[4][:], w3_words, 4, 6)
        load_words(pairs3[2][:], w3_words, 2, 4)
        load_words(pairs1[2][:], w1_words, 2, 4)
        load_words(late_words[:, 0:2, :], w1_words, 6, 8)
        load_words(late_words[:, 2:4, :], w3_words, 6, 8)
        permute(pairs1[4], (("a", 4), ("a", 5)))
        nc.gpsimd.tensor_copy(
            spread_moved[:].rearrange("p (j m) -> p j m", j=4), spread[:].rearrange("p (m j) -> p j m", j=4)
        )
        for quadrant in range(4):
            place(quadrant)
        permute(pairs3[4], (("b", 4), ("b", 5)))
        plane2 = keep.tile([P, E, N], U8, name="spread", align_bytes=64)
        words2 = keep.tile([P, E, 2 * N], U8, name="words3_4", align_bytes=64)
        nc.gpsimd.memset(as_words(plane2), 0)
        gates = keep.tile([P, 2 * T + 2 * P], F32, name="spread_moved", align_bytes=64)
        load_plane(plane2, w2_scales, E)
        load_words(words2[:], w2_words, 0, E)
        for tile, pos in zip(positions, (pos1, pos2, pos3, pos4)):
            nc.sync.dma_start(tile[:], pos)
        by_choice = gate.rearrange("r p t -> p r t")
        gates_fused = gates[:, : 2 * T].rearrange("p (r t) -> p r t", r=2)
        gates_first = gates[:, 2 * T :].rearrange("p (r t) -> p r t", r=2)
        nc.sync.dma_start(gates_fused, by_choice[:, 2:, :])
        nc.sync.dma_start(gates_first, by_choice[:, 0:2, :P])

        def interleave(copy, lo, hi):
            copy(x_rows[:, lo:hi, :], x_raw[:, :, lo:hi].rearrange("p j t -> p t j"))

        def quantise_tokens(lo, hi):
            nc.vector.quantize_mx(
                out=x_codes[:, lo:hi].bitcast(FP8X4),
                scales=x_scales[:, lo:hi],
                in_=x_rows[:, lo:hi, :].rearrange("p t j -> p (t j)"),
            )

        interleave(nc.scalar.copy, 0, 128)
        interleave(nc.vector.tensor_copy, 128, 256)
        quantise_tokens(128, 256)
        quantise_tokens(0, 128)
        interleave(nc.scalar.copy, 416, 512)
        interleave(nc.vector.tensor_copy, 256, 384)
        interleave(nc.vector.tensor_copy, 384, 416)
        quantise_tokens(256, 384)
        quantise_tokens(384, 512)

        gathered = {}
        for lo, hi in RUNS:
            codes = keep.tile([P, hi - lo], U32, name=f"codes{lo}", align_bytes=64)
            scales = keep.tile([P, hi - lo], U8, name=f"scales{lo}", align_bytes=64)
            mine = offsets[:, lo // 16 : hi // 16]
            nc.vector.tensor_copy(codes[:], x_codes[:].indirect(mine))
            nc.vector.tensor_copy(scales[:], x_scales[:].indirect(mine))
            for batch in range(lo // P, hi // P):
                cols = slice(batch * P - lo, batch * P - lo + P)
                gathered[batch] = (codes[:, cols], scales[:, cols])

        pair_a = [keep.tile([P, 2, H], F32, name=f"pair_a{e}") for e in range(POOLED)]
        pair_b = [keep.tile([P, 2, H], F32, name=f"pair_b{e}", align_bytes=64) for e in range(POOLED)]
        h_rows = keep.tile([P, E * C * 4], BF16, name="h_rows", align_bytes=64)
        h_own = keep.tile([P, 2, H], BF16, name="h_own", align_bytes=64)
        arrived = {"a": (pairs1, plane1), "b": (pairs3, plane3)}
        placed = {"a": 0, "b": 1}
        number = {}
        waiting = {}
        activated = {}
        hidden = {}
        turned = {}

        def product(matrix, batch, bank_number):
            number[matrix, batch] = bank_number
            bank = psum.tile([P, H], F32, name=f"bank{bank_number}")
            e = batch // 2
            codes, scales = gathered[batch]
            if e < TURNED:
                pairs, plane = arrived[matrix]
                nc.tensor.matmul_mx(
                    out=bank[:],
                    lhsT=codes.bitcast(FP8X4),
                    lhsT_scale=scales,
                    rhs=pairs[e - e % 2][:, e % 2, :].bitcast(FP4X4),
                    rhs_scale=plane[:, e, :],
                    start=True,
                    stop=True,
                )
            else:
                for j in range(4):
                    nc.tensor.matmul_mx(
                        out=bank[:, j * P : (j + 1) * P],
                        lhsT=moved[matrix, e][:, 2 * j * P : 2 * (j + 1) * P].bitcast(FP4X4),
                        lhsT_scale=moved_plane[:, 2 * (e - TURNED) + placed[matrix], j * P : (j + 1) * P],
                        rhs=codes.bitcast(FP8X4),
                        rhs_scale=scales,
                        start=True,
                        stop=True,
                    )
            return bank

        def in_bank(batch, bank):
            if batch < 2 * TURNED:
                return bank[:].rearrange("p (m u d) -> p u m d", u=2, d=2)
            return bank[:].rearrange("p (j s) -> p s j", j=4)

        def in_row(batch, row):
            if batch < 2 * TURNED:
                return row.rearrange("p (u m d) -> p u m d", u=2, d=2)
            return row.rearrange("p (s j) -> p s j", j=4)

        def activate(batch, bank_number):
            a = product("a", batch, bank_number)
            if batch < 2 * POOLED:
                row = pair_a[batch // 2][:, batch % 2, :]
            else:
                own = keep.tile([P, H], F32, name=f"silu{batch}", align_bytes=64)
                row = own[:]
            nc.scalar.activation(in_row(batch, row), in_bank(batch, a), SILU)
            activated[batch] = row

        def linear(batch, bank_number):
            waiting[batch] = product("b", batch, bank_number)

        def unload(batch):
            nc.scalar.copy(in_row(batch, pair_b[batch // 2][:, batch % 2, :]), in_bank(batch, waiting.pop(batch)))

        def multiply(batch):
            if batch < 2 * TURNED:
                h = h_own[:, batch % 2, :]
                hidden[batch] = h
            else:
                start = (2 * PLACES.index(batch // 2) + batch % 2) * H
                h = h_rows[:, start : start + H]
            nc.vector.tensor_tensor(
                in_row(batch, h), in_bank(batch, waiting.pop(batch)), in_row(batch, activated.pop(batch)), MULT
            )

        def multiply_pooled(e, h):
            nc.gpsimd.tensor_tensor(h, pair_b[e][:], pair_a[e][:], MULT)
            hidden[2 * e] = h[:, 0, :]
            hidden[2 * e + 1] = h[:, 1, :]

        def turn(e, bank_number):
            bank = psum.tile([P, 2, 2, P], F32, name=f"bank{bank_number}")
            for s in range(2):
                h = hidden.pop(2 * e + s)
                for u in range(2):
                    nc.tensor.transpose(bank[:, s, u, :], h[:, u * H // 2 : (u + 1) * H // 2].bitcast(F32), ident[:])
            turned[e] = bank

        def empty(e):
            rows = h_rows[:, PLACES.index(e) * C * 4 : (PLACES.index(e) + 1) * C * 4]
            nc.scalar.copy(
                rows.bitcast(F32).rearrange("p (s c u) -> p s c u", s=2, u=2),
                turned.pop(e)[:].rearrange("p s u c -> p s c u"),
            )

        h_first = keep.tile([P, 2, H], BF16, name="h_first", align_bytes=64)
        activate(0, 0)
        for batch in range(3):
            linear(batch, batch + 1)
            unload(batch)
        activate(1, number["b", 0])
        activate(2, number["b", 1])
        multiply_pooled(0, h_first[:])
        columns = keep.tile([P, 2, 8], F32, name="pair_a0")
        with nc.allow_non_contiguous_dma(reason="one gate a partition"):
            for r in range(2):
                nc.sync.dma_start(columns[:, r, 0:3], gate[r, 0, P:].rearrange("(b p) -> p b", b=3))
        permute(late_words, (("a", 6), ("a", 7), ("b", 6), ("b", 7)))
        h_later = keep.tile([P, 4, H], BF16, name="late_words", align_bytes=64)
        activate(3, number["a", 1])
        linear(3, number["b", 2])
        unload(3)
        multiply_pooled(1, h_later[:, 0:2, :])
        activate(4, number["a", 0])
        linear(4, 4)
        unload(4)
        activate(5, 5)
        linear(5, 6)
        unload(5)
        multiply_pooled(2, h_later[:, 2:4, :])
        activate(6, 7)
        linear(6, number["a", 2])
        activate(7, number["a", 3])
        linear(7, number["b", 3])
        activate(8, number["a", 4])
        activate(9, number["b", 4])
        linear(8, number["a", 5])
        linear(9, number["b", 5])
        activate(10, number["a", 6])
        activate(11, number["a", 7])
        multiply(6)
        linear(10, number["a", 8])
        activate(12, number["b", 6])
        multiply(7)
        linear(11, number["a", 9])
        activate(13, number["b", 7])
        multiply(8)
        activate(14, number["a", 10])
        linear(12, number["b", 8])
        multiply(9)
        activate(15, number["a", 11])
        linear(13, number["b", 9])
        multiply(10)
        linear(14, number["b", 10])
        linear(15, number["a", 12])
        multiply(11)
        for batch in range(12, 16):
            multiply(batch)
        turn_order = [e for e in PLACES if e < TURNED]
        for e, result in zip(turn_order, (("a", 13), ("a", 14), ("a", 15), ("b", 12))):
            turn(e, number[result])
        for e in turn_order:
            empty(e)

        y_all = keep.tile([P, S], F32, name="late_words", align_bytes=64)
        h_codes = keep.tile([P, S], U32, name=f"pair_b{POOLED - 1}", align_bytes=64)
        h_scales = keep.tile([P, S], U8, name="silu14", align_bytes=64)
        groups = (
            (0, 2 * C, number["b", 11], nc.scalar.copy),
            (2 * C, 4 * C, number["b", 13], nc.scalar.copy),
            (4 * C, 6 * C, number["b", 14], nc.vector.tensor_copy),
            (6 * C, 7 * C, number["b", 15], nc.scalar.copy),
            (7 * C, 7 * C + P, number["a", 13], nc.scalar.copy),
            (7 * C + P, 8 * C, number["a", 14], nc.scalar.copy),
        )
        for lo, hi, bank_number, copy in groups:
            nc.vector.quantize_mx(
                out=h_codes[:, lo:hi].bitcast(FP8X4), scales=h_scales[:, lo:hi], in_=h_rows[:, lo * 4 : hi * 4]
            )
        results = []
        for lo, hi, bank_number, copy in groups:
            width = min(C, hi - lo)
            y = psum.tile([P, (hi - lo) // width, width], F32, name=f"bank{bank_number}")
            for i, start in enumerate(range(lo, hi, width)):
                mine = slice(start, start + width)
                nc.tensor.matmul_mx(
                    out=y[:, i, :],
                    lhsT=words2[:, PLACES[start // C], :].bitcast(FP4X4),
                    lhsT_scale=plane2[:, PLACES[start // C], :],
                    rhs=h_codes[:, mine].bitcast(FP8X4),
                    rhs_scale=h_scales[:, mine],
                    start=True,
                    stop=True,
                )
            results.append(y)
        by_expert = y_all[:].rearrange("p (e c) -> p e c", c=C)
        for (lo, hi, bank_number, copy), y in zip(groups, results):
            low, high = PLACES[lo // C], PLACES[(hi - 1) // C]
            copy(by_expert[:, low : high + 1 : max(high - low, 1), lo % C : (hi - 1) % C + 1], y[:])

        blocks = T // P - 1
        first, rest = slice(0, P), slice(P, T)
        total = keep.tile([P, T], F32, name="total")
        fetched = keep.tile([P, 2, T + P], F32, name="fetched")
        both = keep.tile([P, T + P], F32, name="both")
        gated = keep.tile([P, 2, blocks, P], F32, name="gated")
        shared = psum.tile([P, blocks, P], F32, name="bank0")
        single = [psum.tile([P, P], F32, name=f"bank{1 + b}") for b in range(blocks)]
        across = ([shared[:, b, :] for b in range(blocks)], [bank[:] for bank in single])
        back = [psum.tile([P, P], F32, name=f"bank{1 + blocks + b}") for b in range(blocks)]

        def slots_of(r, cols):
            return y_all[:].indirect(positions[r][:, cols.start // 16 : cols.stop // 16])

        for r in range(2):
            plain = keep.tile([P, blocks * P], F32, name=f"plain{r}")
            nc.scalar.activation(plain[:], slots_of(r, rest), COPY)
            for b in range(blocks):
                nc.tensor.transpose(across[r][b], plain[:, b * P : (b + 1) * P], ident[:])
        for r in range(2):
            for b in range(blocks):
                nc.scalar.activation(gated[:, r, b, :], across[r][b], COPY, scale=columns[:, r, b : b + 1])
                nc.tensor.matmul(
                    back[b][:], gated[:, r, b, :], ident[:], start=(r == 0), stop=(r == 1), is_transpose=True
                )
        for r in range(2):
            nc.vector.tensor_tensor(fetched[:, r, :T], slots_of(2 + r, slice(0, T)), gates_fused[:, r, :], MULT)
        for r in range(2):
            nc.vector.tensor_tensor(fetched[:, r, T:], slots_of(r, first), gates_first[:, r, :], MULT)
        nc.vector.tensor_tensor(both[:, :T], fetched[:, 0, :T], fetched[:, 1, :T], ADD)
        nc.vector.tensor_tensor(both[:, T:], fetched[:, 0, T:], fetched[:, 1, T:], ADD)
        for b in range(blocks):
            cols = slice((b + 1) * P, (b + 2) * P)
            nc.vector.tensor_tensor(total[:, cols], back[b][:], both[:, cols], ADD)
            if b == 0:
                nc.vector.tensor_tensor(total[:, first], both[:, first], both[:, T:], ADD)
                cols = slice(0, 2 * P)
            nc.sync.dma_start(out[:, cols], total[:, cols])
